import numpy as np
import ml_dtypes


def mxq(x, axis, fmt="e4m3"):
    dtype, down = {"e4m3": (ml_dtypes.float8_e4m3fn, 7), "e5m2": (ml_dtypes.float8_e5m2, 14)}[fmt]
    v = np.moveaxis(np.asarray(x, np.float32).astype(ml_dtypes.bfloat16).astype(np.float64), axis, -1)
    blocks = v.reshape(v.shape[:-1] + (-1, 32))
    amax = np.abs(blocks).max(-1, keepdims=True)
    byte = np.maximum(np.where(amax > 0, np.frexp(amax)[1] - 1 + 127, 0) - down, 1)
    scale = np.exp2(byte - 127.0)
    codes = (blocks / scale).astype(np.float32).astype(dtype).astype(np.float64)
    return np.moveaxis((codes * scale).reshape(v.shape), -1, axis)


WIDE = False


def mx_kscale(k):
    if not WIDE:
        return np.ones(k)
    levels = np.array([24, -24, 12, -12, 0])
    if k % 512:
        return np.exp2(np.random.permutation(np.resize(levels, k // 32))).repeat(32)
    a = np.empty((k // 512, 16))
    for p in range(k // 512):
        a[p, :8] = np.random.permutation(np.resize(levels, 8))
        for g in range(8):
            far = levels[np.abs(levels - a[p, g]) >= 10]
            a[p, g + 8] = far[np.random.randint(len(far))]
    return np.exp2(a.ravel()).repeat(32)


def f64(x):
    return np.asarray(x).astype(np.float64)


def striped8(idx):
    return np.concatenate([v.reshape(-1, 16).T for v in idx]).astype(np.uint16)


def unstriped8(offs):
    return np.stack([offs[16 * g:16 * g + 16].T.reshape(-1) for g in range(8)]).astype(np.int64)


E2M1 = np.array([0.0, 0.5, 1.0, 1.5, 2.0, 3.0, 4.0, 6.0, -0.0, -0.5, -1.0, -1.5, -2.0, -3.0, -4.0, -6.0])


def pack_weight(w, fmt):
    k, n = w.shape
    w = f64(np.asarray(w, np.float32).astype(ml_dtypes.bfloat16)).reshape(k // 32, 32, n)
    amax = np.abs(w).max(1)
    if fmt == "e4m3":
        byte = np.frexp(amax)[1] - 1 + 127 - 7
    else:
        mant, ex = np.frexp(amax / 6.0)
        byte = np.where(mant > 0.5, ex, ex - 1) + 127
    byte = np.clip(np.where(amax > 0, byte, 1), 1, 254)
    scaled = (w * np.exp2(127.0 - byte)[:, None, :]).reshape(k, n).astype(np.float32)
    by_word = np.ascontiguousarray(scaled.reshape(k // 512, 128, 4, n).transpose(0, 1, 3, 2))
    if fmt == "e4m3":
        words = by_word.astype(ml_dtypes.float8_e4m3fn).view(np.uint8)
    else:
        c = by_word.astype(ml_dtypes.float4_e2m1fn).view(np.uint8) & 0xF
        words = (c[..., 0::2] | (c[..., 1::2] << 4)).reshape(k // 512, 128, 2 * n)
    return np.ascontiguousarray(words), np.ascontiguousarray(byte.astype(np.uint8).reshape(k // 512, 16, n))


def unpack_weight(words, scales, fmt):
    g, _, n = scales.shape
    words = np.ascontiguousarray(words).reshape(g, 128, n, -1)
    if fmt == "e4m3":
        vals = words.view(ml_dtypes.float8_e4m3fn).astype(np.float64)
    else:
        nib = np.empty((g, 128, n, 4), np.uint8)
        nib[..., 0::2] = words & 0xF
        nib[..., 1::2] = words >> 4
        vals = E2M1[nib]
    vals = vals * np.repeat(np.exp2(scales.astype(np.float64) - 127.0), 8, axis=1)[..., None]
    return vals.transpose(0, 1, 3, 2).reshape(g * 512, n)


K, L, N, T, J = 512, 512, 512, 2048, 1024


def setup_inputs():
    n = np.random.standard_normal
    s = mx_kscale(K)[:, None]
    s2 = mx_kscale(L)[:, None]
    p_wt = pack_weight(n((K, N)) / np.sqrt(K) / s, "e2m1")
    p_wx = pack_weight(n((L, N)) / np.sqrt(L) / s2, "e4m3")
    return {
        "xT": (n((K, T)) * s).astype(np.float32),
        "wgt": np.repeat(np.random.uniform(0.5, 2.0, (8, J)), 16, axis=0).astype(np.float32),
        "wt_words": p_wt[0],
        "wt_scales": p_wt[1],
        "c": (n((L, J)) * s2).astype(np.float32),
        "wx_words": p_wx[0],
        "wx_scales": p_wx[1],
        "b": (0.3 * n(N)).astype(np.float32),
        "wgo": np.repeat(np.random.uniform(0.5, 2.0, (8, J)), 16, axis=0).astype(np.float32),
        "offs": striped8(np.stack([np.random.permutation(T)[:J] for _ in range(8)])),
        "offs2": striped8(np.stack([np.random.permutation(T)[:J] for _ in range(8)])),
    }


def reference(xT, wgt, wt_words, wt_scales, c, wx_words, wx_scales, b, wgo, offs, offs2):
    idx = unstriped8(offs)
    idx2 = unstriped8(offs2)
    rows = np.arange(K)
    xg = f64(wgt)[rows // 4 % 128] * f64(xT)[rows[:, None], idx[rows % 512 // 64]]
    xT_ = mxq(xg, 0, "e4m3")
    wt_ = unpack_weight(wt_words, wt_scales, "e2m1")
    c_q_ = mxq(f64(c), 0, "e4m3")
    c_r_ = mxq(f64(c) - c_q_, 0, "e4m3")
    wx_ = unpack_weight(wx_words, wx_scales, "e4m3")
    y = wt_.T @ xT_ + wx_.T @ c_q_ + wx_.T @ c_r_
    out = np.zeros((N, T))
    rows = np.arange(N)
    out[rows[:, None], idx2[rows % 128 // 16]] = f64(wgo)[rows % 128] * (y + f64(b)[:, None])
    return out

@@ -1,0 +1,262 @@
+from contextlib import ExitStack
+
+import concourse.mybir as mybir
+from concourse.masks import make_identity
+
+K, L, N, T, J = 512, 512, 512, 2048, 1024
+FLOPS = 4 * 2 * 512 * 512 * 1024
+
+F32 = mybir.dt.float32
+BF16 = mybir.dt.bfloat16
+I32 = mybir.dt.int32
+U32 = mybir.dt.uint32
+U16 = mybir.dt.uint16
+U8 = mybir.dt.uint8
+FP8X4 = mybir.dt.float8_e4m3fn_x4
+FP4X4 = mybir.dt.float4_e2m1fn_x4
+MULT = mybir.AluOpType.mult
+SUB = mybir.AluOpType.subtract
+IDENT = mybir.ActivationFunctionType.Identity
+
+P = 128
+PACK = 4
+HALF = 512
+CHUNK = 256
+STRIP = 128
+EARLY = 768
+LIST_COLS = HALF // 16
+
+
+def tile_list_scatb_kernel(
+    tc, xT, wgt, wt_words, wt_scales, c, wx_words, wx_scales, b, wgo, offs, offs2, out
+):
+    nc = tc.nc
+    with ExitStack() as ctx:
+        lists = ctx.enter_context(tc.tile_pool(name="lists", bufs=1))
+        keep = ctx.enter_context(tc.tile_pool(name="keep", bufs=1))
+        over = ctx.enter_context(tc.tile_pool(name="over", bufs=1))
+        ps_dq = ctx.enter_context(tc.psum_pool(name="ps_dq", bufs=4))
+        ps_y = ctx.enter_context(tc.psum_pool(name="ps_y", bufs=4))
+
+        def held(name, shape, dtype, slot=None):
+            return keep.tile(shape, dtype, name=name, tag=slot or name, align_bytes=64)
+
+        picks = lists.tile([P, J // 16], U16, name="picks")
+        places = lists.tile([P, J // 16], U16, name="places")
+        halves = range(J // HALF)
+        chunks = range(J // CHUNK)
+        tiles = range(N // P)
+
+        x_pl = [held(f"x_pl{i}", [P, T], F32) for i in range(PACK)]
+        c_raw = [held(f"c_raw{q}", [P, PACK, CHUNK], F32) for q in chunks]
+        wgt_a = held("wgt_a", [P, EARLY], F32)
+        wgt_b = held("wgt_b", [P, J - EARLY], F32)
+        wgo_sb = [held(f"wgo_sb{h}", [P, HALF], F32) for h in halves]
+        wt_w = held("wt_w", [P, 2 * N], U8)
+        wx_w = held("wx_w", [P, N], U32)
+        wt_s = held("wt_s", [P, N], U8)
+        wx_s = held("wx_s", [P, N], U8)
+        bias = held("bias", [P, N // P], F32)
+        win = {t: held(f"win{t}", [P, T], F32) for t in (0, 1)}
+        eye = held("eye", [P, P], BF16)
+        sel = held("sel", [P, PACK, P, PACK], BF16)
+        sel_w = held("sel_w", [P, PACK * P], U32)
+        sel_s = held("sel_s", [P, PACK * P], U8)
+        names = ("x", "cq", "cr")
+        own = (("x", 0), ("x", 1), ("cq", 0), ("cq", 1), ("cr", 0), ("cr", 2), ("cr", 3))
+        grouped = {(o, q): held(f"g_{o}{q}", [P, CHUNK, PACK], BF16)[:] for o, q in own}
+        grouped["cr", 1] = over.tile([P, CHUNK, PACK], BF16, name="g_cr1", align_bytes=64, offset=4 * T - 1024)[:]
+        words = {(o, h): held(f"w_{o}{h}", [P, HALF], U32) for o in names for h in halves}
+        scales = {(o, h): held(f"s_{o}{h}", [P, HALF], U8) for o in names for h in halves}
+        ys, acc = {}, {}
+
+        x_src = xT.rearrange("(p i) t -> i p t", i=PACK)
+        c_src = c.rearrange("(p i) j -> p i j", i=PACK)
+
+        def load_c(q):
+            nc.sync.dma_start(out=c_raw[q][:], in_=c_src[:, :, q * CHUNK : (q + 1) * CHUNK])
+
+        make_identity(nc, eye[:])
+        load_c(0)
+        load_c(1)
+        nc.sync.dma_start(picks[:], offs)
+        nc.sync.dma_start(out=wgt_a[:], in_=wgt[:, 0:EARLY])
+        for i in range(PACK):
+            nc.sync.dma_start(out=x_pl[i][:], in_=x_src[i])
+        nc.sync.dma_start(out=wgt_b[:], in_=wgt[:, EARLY:J])
+        nc.sync.dma_start(out=wx_w[:].bitcast(I32), in_=wx_words[0].rearrange("p n t -> p (n t)").bitcast(I32))
+        nc.sync.dma_start(out=wt_w[:].bitcast(I32), in_=wt_words[0].bitcast(I32))
+        for plane, src in ((wx_s, wx_scales), (wt_s, wt_scales)):
+            nc.gpsimd.memset(plane[:].bitcast(I32), 0)
+            for quad in range(4):
+                nc.sync.dma_start(
+                    out=plane[32 * quad : 32 * quad + 4, :].bitcast(I32),
+                    in_=src[0, 4 * quad : 4 * quad + 4, :].bitcast(I32),
+                )
+        with nc.allow_non_contiguous_dma(reason="one bias value a partition"):
+            nc.sync.dma_start(out=bias[:], in_=b.rearrange("(t p) -> p t", p=P))
+        nc.sync.dma_start(out=wgo_sb[0][:], in_=wgo[:, 0:HALF])
+        nc.sync.dma_start(places[:], offs2)
+        load_c(2)
+        load_c(3)
+        nc.sync.dma_start(out=wgo_sb[1][:], in_=wgo[:, HALF:J])
+
+        nc.vector.memset(sel[:].rearrange("p i m t -> p (i m t)").bitcast(I32), 0)
+        for i in range(PACK):
+            nc.scalar.copy(out=sel[:, i, :, i], in_=eye[:])
+        nc.vector.memset(win[0][:], 0.0)
+        nc.vector.memset(win[1][:], 0.0)
+        nc.vector.quantize_mx(
+            out=sel_w[:].bitcast(FP8X4), scales=sel_s[:], in_=sel[:].rearrange("p i m t -> p (i m t)")
+        )
+
+        def chunk_cols(q):
+            lo = q * CHUNK % HALF
+            return q * CHUNK // HALF, slice(lo, lo + CHUNK)
+
+        def interleave(dst, src):
+            nc.scalar.copy(
+                out=dst.rearrange("p (a e) t -> p a t e", e=4),
+                in_=src.rearrange("p t (a e) -> p a t e", e=4),
+            )
+
+        def quantize(o, q):
+            h, cols = chunk_cols(q)
+            nc.vector.quantize_mx(
+                out=words[o, h][:, cols].bitcast(FP8X4),
+                scales=scales[o, h][:, cols],
+                in_=grouped[o, q].rearrange("p j t -> p (j t)"),
+            )
+
+        def residual(q, s):
+            h, cols = chunk_cols(q)
+            strip = slice(s * STRIP, (s + 1) * STRIP)
+            hcols = slice(cols.start + strip.start, cols.start + strip.stop)
+            dq = ps_dq.tile([P, PACK, STRIP], F32, name="dq")
+            for i in range(PACK):
+                nc.tensor.matmul_mx(
+                    out=dq[:, i, :],
+                    lhsT=sel_w[:, i * P : (i + 1) * P].bitcast(FP8X4),
+                    lhsT_scale=sel_s[:, i * P : (i + 1) * P],
+                    rhs=words["cq", h][:, hcols].bitcast(FP8X4),
+                    rhs_scale=scales["cq", h][:, hcols],
+                    start=True,
+                    stop=True,
+                )
+            nc.vector.tensor_tensor(
+                out=grouped["cr", q][:, strip, :],
+                in0=c_raw[q][:, :, strip].rearrange("p t j -> p j t"),
+                in1=dq[:].rearrange("p t j -> p j t"),
+                op=SUB,
+            )
+
+        def gather(xg, i, lo, hi):
+            base, factors = (0, wgt_a) if hi <= EARLY else (EARLY, wgt_b)
+            nc.vector.tensor_tensor(
+                xg[:, i, lo - base : hi - base],
+                x_pl[i][:].indirect(picks[:, lo // 16 : hi // 16]),
+                factors[:, lo - base : hi - base],
+                MULT,
+            )
+
+        def interleave_x(xg, q):
+            lo = q * CHUNK % EARLY
+            interleave(grouped["x", q], xg[:, :, lo : lo + CHUNK])
+
+        def project(t, h):
+            acc[t, h] = ps_y.tile([P, HALF], F32, name="acc")
+            ncols = slice(t * P, (t + 1) * P)
+            for o in ("cq", "cr"):
+                nc.tensor.matmul_mx(
+                    out=acc[t, h][:],
+                    lhsT=wx_w[:, ncols].bitcast(FP8X4),
+                    lhsT_scale=wx_s[:, ncols],
+                    rhs=words[o, h][:].bitcast(FP8X4),
+                    rhs_scale=scales[o, h][:],
+                    start=(o == "cq"),
+                    stop=False,
+                )
+            nc.tensor.matmul_mx(
+                out=acc[t, h][:],
+                lhsT=wt_w[:, 2 * t * P : 2 * (t + 1) * P].bitcast(FP4X4),
+                lhsT_scale=wt_s[:, ncols],
+                rhs=words["x", h][:].bitcast(FP8X4),
+                rhs_scale=scales["x", h][:],
+                start=False,
+                stop=True,
+            )
+
+        def add_bias(t, h, slot=None):
+            ys[t, h] = held(f"ys{t}_{h}", [P, HALF], F32, slot=slot)
+            nc.scalar.activation(out=ys[t, h][:], in_=acc[t, h][:], func=IDENT, bias=bias[:, t : t + 1], scale=1.0)
+
+        def scatter(t, h):
+            nc.vector.tensor_tensor(
+                win[t][:].indirect(places[:, h * LIST_COLS : (h + 1) * LIST_COLS]),
+                ys[t, h][:],
+                wgo_sb[h][:],
+                MULT,
+            )
+
+        interleave(grouped["cq", 0], c_raw[0][:])
+        interleave(grouped["cq", 1], c_raw[1][:])
+        quantize("cq", 0)
+        residual(0, 0)
+        quantize("cq", 1)
+        residual(0, 1)
+        residual(1, 0)
+        quantize("cr", 0)
+        residual(1, 1)
+        xg = held("xg", [P, PACK, EARLY], F32, slot="c_raw1")
+        gather(xg, 0, 0, EARLY)
+        quantize("cr", 1)
+        for t in (2, 3):
+            win[t] = over.tile([P, T], F32, name=f"win{t}", align_bytes=64, offset=(t - 2) * 4 * T)
+            nc.gpsimd.memset(win[t][:], 0.0)
+        gather(xg, 1, 0, EARLY)
+        gather(xg, 2, 0, EARLY)
+        gather(xg, 3, 0, CHUNK)
+        interleave_x(xg, 0)
+        gather(xg, 3, CHUNK, HALF)
+        interleave_x(xg, 1)
+        gather(xg, 3, HALF, EARLY)
+        quantize("x", 0)
+        xg_last = held("xg_last", [P, PACK, J - EARLY], F32, slot="g_x0")
+        gather(xg_last, 0, EARLY, J)
+        gather(xg_last, 1, EARLY, J)
+        quantize("x", 1)
+        gather(xg_last, 2, EARLY, J)
+        gather(xg_last, 3, EARLY, J)
+        for t in tiles:
+            project(t, 0)
+        add_bias(0, 0)
+        add_bias(1, 0)
+        late = held("late", [P, 4, CHUNK, PACK], BF16, slot="w_x0")
+        for n, key in enumerate((("cq", 2), ("cq", 3), ("x", 2), ("x", 3))):
+            grouped[key] = late[:, n, :, :]
+        interleave(grouped["cq", 2], c_raw[2][:])
+        interleave(grouped["cq", 3], c_raw[3][:])
+        interleave_x(xg, 2)
+        interleave_x(xg_last, 3)
+        scatter(0, 0)
+        scatter(1, 0)
+        quantize("cq", 2)
+        quantize("cq", 3)
+        quantize("x", 2)
+        quantize("x", 3)
+        add_bias(2, 0, slot="w_x0")
+        residual(2, 0)
+        residual(2, 1)
+        residual(3, 0)
+        quantize("cr", 2)
+        add_bias(3, 0, slot="g_cr2")
+        residual(3, 1)
+        scatter(2, 0)
+        quantize("cr", 3)
+        scatter(3, 0)
+        for t in tiles:
+            project(t, 1)
+            add_bias(t, 1)
+        for t in tiles:
+            scatter(t, 1)
+            nc.sync.dma_start(out=out[t * P : (t + 1) * P, :], in_=win[t][:])

@@ -16,6 +16,7 @@ FP8X4 = mybir.dt.float8_e4m3fn_x4
 FP4X4 = mybir.dt.float4_e2m1fn_x4
 MULT = mybir.AluOpType.mult
 SUB = mybir.AluOpType.subtract
+COPY = mybir.ActivationFunctionType.Copy
 IDENT = mybir.ActivationFunctionType.Identity
 
 P = 128
@@ -41,6 +42,9 @@ def tile_list_scatb_kernel(
         def held(name, shape, dtype, slot=None):
             return keep.tile(shape, dtype, name=name, tag=slot or name, align_bytes=64)
 
+        def shared(name, shape, dtype, offset):
+            return over.tile(shape, dtype, name=name, align_bytes=64, offset=offset)
+
         picks = lists.tile([P, J // 16], U16, name="picks")
         places = lists.tile([P, J // 16], U16, name="places")
         halves = range(J // HALF)
@@ -58,17 +62,17 @@ def tile_list_scatb_kernel(
         wx_s = held("wx_s", [P, N], U8)
         bias = held("bias", [P, N // P], F32)
         win = {t: held(f"win{t}", [P, T], F32) for t in (0, 1)}
-        eye = held("eye", [P, P], BF16)
-        sel = held("sel", [P, PACK, P, PACK], BF16)
-        sel_w = held("sel_w", [P, PACK * P], U32)
-        sel_s = held("sel_s", [P, PACK * P], U8)
+        eye = held("eye", [P, P], F32)
+        sel = held("sel", [P, P * PACK], BF16)
+        sel_w = held("sel_w", [P, PACK, P], U32)
+        sel_s = held("sel_s", [P, P], U8)
         names = ("x", "cq", "cr")
-        own = (("x", 0), ("x", 1), ("cq", 0), ("cq", 1), ("cr", 0), ("cr", 2), ("cr", 3))
+        own = (("cq", 0), ("cq", 1), ("cr", 0), ("x", 1), ("cr", 2), ("cr", 3))
         grouped = {(o, q): held(f"g_{o}{q}", [P, CHUNK, PACK], BF16)[:] for o, q in own}
-        grouped["cr", 1] = over.tile([P, CHUNK, PACK], BF16, name="g_cr1", align_bytes=64, offset=4 * T - 1024)[:]
-        words = {(o, h): held(f"w_{o}{h}", [P, HALF], U32) for o in names for h in halves}
+        words = {(o, h): held(f"w_{o}{h}", [P, HALF], U32) for o in names for h in halves if (o, h) != ("x", 0)}
+        words["x", 0] = shared("w_x0", [P, HALF], U32, 9216)
         scales = {(o, h): held(f"s_{o}{h}", [P, HALF], U8) for o in names for h in halves}
-        ys, acc = {}, {}
+        ys, acc, dq, neg, left, left_bf, back = {}, {}, {}, {}, {}, {}, {}
 
         x_src = xT.rearrange("(p i) t -> i p t", i=PACK)
         c_src = c.rearrange("(p i) j -> p i j", i=PACK)
@@ -76,39 +80,55 @@ def tile_list_scatb_kernel(
         def load_c(q):
             nc.sync.dma_start(out=c_raw[q][:], in_=c_src[:, :, q * CHUNK : (q + 1) * CHUNK])
 
-        make_identity(nc, eye[:])
-        load_c(0)
-        load_c(1)
-        nc.sync.dma_start(picks[:], offs)
-        nc.sync.dma_start(out=wgt_a[:], in_=wgt[:, 0:EARLY])
-        for i in range(PACK):
-            nc.sync.dma_start(out=x_pl[i][:], in_=x_src[i])
-        nc.sync.dma_start(out=wgt_b[:], in_=wgt[:, EARLY:J])
-        nc.sync.dma_start(out=wx_w[:].bitcast(I32), in_=wx_words[0].rearrange("p n t -> p (n t)").bitcast(I32))
-        nc.sync.dma_start(out=wt_w[:].bitcast(I32), in_=wt_words[0].bitcast(I32))
-        for plane, src in ((wx_s, wx_scales), (wt_s, wt_scales)):
-            nc.gpsimd.memset(plane[:].bitcast(I32), 0)
+        def load_scales(plane, src):
             for quad in range(4):
                 nc.sync.dma_start(
                     out=plane[32 * quad : 32 * quad + 4, :].bitcast(I32),
                     in_=src[0, 4 * quad : 4 * quad + 4, :].bitcast(I32),
                 )
+
+        nc.gpsimd.memset(sel[:], 0.0)
+        nc.gpsimd.affine_select(
+            out=sel[:],
+            in_=sel[:],
+            pattern=[[1, PACK * P]],
+            compare_op=mybir.AluOpType.not_equal,
+            fill=1.0,
+            base=0,
+            channel_multiplier=-PACK,
+        )
+        make_identity(nc, eye[:])
+        nc.vector.memset(wx_s[:].bitcast(I32), 0)
+        nc.vector.memset(wt_s[:].bitcast(I32), 0)
+        load_c(0)
+        load_c(1)
+        nc.sync.dma_start(picks[:], offs)
+        nc.sync.dma_start(out=wgt_a[:], in_=wgt[:, 0:EARLY])
+        load_scales(wx_s, wx_scales)
+        for i in range(PACK):
+            nc.sync.dma_start(out=x_pl[i][:], in_=x_src[i])
+        load_scales(wt_s, wt_scales)
+        nc.sync.dma_start(out=wgt_b[:], in_=wgt[:, EARLY:J])
+        nc.sync.dma_start(out=wx_w[:].bitcast(I32), in_=wx_words[0].rearrange("p n t -> p (n t)").bitcast(I32))
+        nc.sync.dma_start(out=wt_w[:].bitcast(I32), in_=wt_words[0].bitcast(I32))
+        load_c(2)
         with nc.allow_non_contiguous_dma(reason="one bias value a partition"):
             nc.sync.dma_start(out=bias[:], in_=b.rearrange("(t p) -> p t", p=P))
         nc.sync.dma_start(out=wgo_sb[0][:], in_=wgo[:, 0:HALF])
         nc.sync.dma_start(places[:], offs2)
-        load_c(2)
         load_c(3)
         nc.sync.dma_start(out=wgo_sb[1][:], in_=wgo[:, HALF:J])
 
-        nc.vector.memset(sel[:].rearrange("p i m t -> p (i m t)").bitcast(I32), 0)
-        for i in range(PACK):
-            nc.scalar.copy(out=sel[:, i, :, i], in_=eye[:])
-        nc.vector.memset(win[0][:], 0.0)
-        nc.vector.memset(win[1][:], 0.0)
+        nc.vector.memset(sel_w[:, 1:PACK, :], 0)
         nc.vector.quantize_mx(
-            out=sel_w[:].bitcast(FP8X4), scales=sel_s[:], in_=sel[:].rearrange("p i m t -> p (i m t)")
+            out=sel_w[:, 0, :].bitcast(FP8X4), scales=sel_s[:], in_=sel[:]
         )
+        for i in range(1, PACK):
+            nc.vector.tensor_copy(
+                out=sel_w[:, i, :].bitcast(U8)[:, i::PACK], in_=sel_w[:, 0, :].bitcast(U8)[:, 0::PACK]
+            )
+        for t in range(2):
+            nc.vector.memset(win[t][:], 0.0)
 
         def chunk_cols(q):
             lo = q * CHUNK % HALF
@@ -128,26 +148,60 @@ def tile_list_scatb_kernel(
                 in_=grouped[o, q].rearrange("p j t -> p (j t)"),
             )
 
-        def residual(q, s):
-            h, cols = chunk_cols(q)
-            strip = slice(s * STRIP, (s + 1) * STRIP)
-            hcols = slice(cols.start + strip.start, cols.start + strip.stop)
-            dq = ps_dq.tile([P, PACK, STRIP], F32, name="dq")
+        def decode(s):
+            h, lo = divmod(s * STRIP, HALF)
+            dq[s] = ps_dq.tile([P, PACK, STRIP], F32, name="dq", tag="bank")
             for i in range(PACK):
                 nc.tensor.matmul_mx(
-                    out=dq[:, i, :],
-                    lhsT=sel_w[:, i * P : (i + 1) * P].bitcast(FP8X4),
-                    lhsT_scale=sel_s[:, i * P : (i + 1) * P],
-                    rhs=words["cq", h][:, hcols].bitcast(FP8X4),
-                    rhs_scale=scales["cq", h][:, hcols],
+                    out=dq[s][:, i, :],
+                    lhsT=sel_w[:, i, :].bitcast(FP8X4),
+                    lhsT_scale=sel_s[:],
+                    rhs=words["cq", h][:, lo : lo + STRIP].bitcast(FP8X4),
+                    rhs_scale=scales["cq", h][:, lo : lo + STRIP],
                     start=True,
                     stop=True,
                 )
+
+        def subtract_on_vector(s):
+            q, lo = divmod(s * STRIP, CHUNK)
             nc.vector.tensor_tensor(
-                out=grouped["cr", q][:, strip, :],
-                in0=c_raw[q][:, :, strip].rearrange("p t j -> p j t"),
-                in1=dq[:].rearrange("p t j -> p j t"),
+                out=grouped["cr", q][:, lo : lo + STRIP, :].rearrange("p (a e) t -> p a t e", e=4),
+                in0=c_raw[q][:, :, lo : lo + STRIP].rearrange("p t (a e) -> p a t e", e=4),
+                in1=dq[s][:].rearrange("p t (a e) -> p a t e", e=4),
                 op=SUB,
+            )
+
+        def negate(s):
+            neg[s] = held(f"neg{s}", [P, PACK, STRIP], F32)
+            nc.scalar.activation(out=neg[s][:], in_=dq[s][:], func=COPY, scale=-1.0)
+
+        def subtract(s):
+            q, lo = divmod(s * STRIP, CHUNK)
+            left[s] = ps_dq.tile([STRIP, PACK, P], F32, name="left", tag="bank")
+            for i in range(PACK):
+                terms = (neg[s][:, i, :], c_raw[q][:, i, lo : lo + STRIP])
+                for n, term in enumerate(terms):
+                    nc.tensor.matmul(
+                        out=left[s][:, i, :], lhsT=term, rhs=eye[:], start=(n == 0), stop=(n == 1), is_transpose=True
+                    )
+
+        def round_left(s):
+            shape = [STRIP, 2, P, 2]
+            left_bf[s] = held(f"left_bf{s}", shape, BF16)
+            nc.scalar.copy(out=left_bf[s][:], in_=left[s][:].rearrange("j (u e) p -> j u p e", u=2))
+
+        def turn_back(s):
+            q, r = divmod(s, 2)
+            if r == 0:
+                back[q] = ps_dq.tile([P, 2, 2, STRIP], F32, name="back", tag="bank")
+            pairs = left_bf[s][:].rearrange("j u p e -> j (u p e)").bitcast(F32)
+            for u in range(2):
+                nc.tensor.transpose(back[q][:, r, u, :], pairs[:, u * P : (u + 1) * P], eye[:])
+
+        def regroup(q):
+            nc.scalar.copy(
+                out=grouped["cr", q].bitcast(F32).rearrange("p (r j) u -> p r j u", r=2),
+                in_=back[q][:].rearrange("p r u j -> p r j u"),
             )
 
         def gather(xg, i, lo, hi):
@@ -163,28 +217,23 @@ def tile_list_scatb_kernel(
             lo = q * CHUNK % EARLY
             interleave(grouped["x", q], xg[:, :, lo : lo + CHUNK])
 
-        def project(t, h):
+        def project(t, h, order):
             acc[t, h] = ps_y.tile([P, HALF], F32, name="acc")
             ncols = slice(t * P, (t + 1) * P)
-            for o in ("cq", "cr"):
+            for o in order:
+                if o == "x":
+                    w, ws = wt_w[:, 2 * t * P : 2 * (t + 1) * P].bitcast(FP4X4), wt_s[:, ncols]
+                else:
+                    w, ws = wx_w[:, ncols].bitcast(FP8X4), wx_s[:, ncols]
                 nc.tensor.matmul_mx(
                     out=acc[t, h][:],
-                    lhsT=wx_w[:, ncols].bitcast(FP8X4),
-                    lhsT_scale=wx_s[:, ncols],
+                    lhsT=w,
+                    lhsT_scale=ws,
                     rhs=words[o, h][:].bitcast(FP8X4),
                     rhs_scale=scales[o, h][:],
-                    start=(o == "cq"),
-                    stop=False,
+                    start=(o == order[0]),
+                    stop=(o == order[-1]),
                 )
-            nc.tensor.matmul_mx(
-                out=acc[t, h][:],
-                lhsT=wt_w[:, 2 * t * P : 2 * (t + 1) * P].bitcast(FP4X4),
-                lhsT_scale=wt_s[:, ncols],
-                rhs=words["x", h][:].bitcast(FP8X4),
-                rhs_scale=scales["x", h][:],
-                start=False,
-                stop=True,
-            )
 
         def add_bias(t, h, slot=None):
             ys[t, h] = held(f"ys{t}_{h}", [P, HALF], F32, slot=slot)
@@ -198,20 +247,29 @@ def tile_list_scatb_kernel(
                 MULT,
             )
 
+        def tile_of(name, offset):
+            return shared(name, [P, CHUNK, PACK], BF16, offset)[:]
+
+        grouped["cr", 1] = tile_of("g_cr1", 16384 + 4 * T - 1024)
+        grouped["x", 0] = tile_of("g_x0", 3072)
         interleave(grouped["cq", 0], c_raw[0][:])
         interleave(grouped["cq", 1], c_raw[1][:])
         quantize("cq", 0)
-        residual(0, 0)
+        decode(0)
+        decode(1)
+        subtract_on_vector(0)
         quantize("cq", 1)
-        residual(0, 1)
-        residual(1, 0)
+        decode(2)
+        decode(3)
+        subtract_on_vector(1)
+        subtract_on_vector(2)
         quantize("cr", 0)
-        residual(1, 1)
+        subtract_on_vector(3)
         xg = held("xg", [P, PACK, EARLY], F32, slot="c_raw1")
         gather(xg, 0, 0, EARLY)
         quantize("cr", 1)
         for t in (2, 3):
-            win[t] = over.tile([P, T], F32, name=f"win{t}", align_bytes=64, offset=(t - 2) * 4 * T)
+            win[t] = shared(f"win{t}", [P, T], F32, 16384 + (t - 2) * 4 * T)
             nc.gpsimd.memset(win[t][:], 0.0)
         gather(xg, 1, 0, EARLY)
         gather(xg, 2, 0, EARLY)
@@ -221,41 +279,54 @@ def tile_list_scatb_kernel(
         interleave_x(xg, 1)
         gather(xg, 3, HALF, EARLY)
         quantize("x", 0)
-        xg_last = held("xg_last", [P, PACK, J - EARLY], F32, slot="g_x0")
+        xg_last = shared("xg_last", [P, PACK, J - EARLY], F32, 0)
         gather(xg_last, 0, EARLY, J)
         gather(xg_last, 1, EARLY, J)
         quantize("x", 1)
         gather(xg_last, 2, EARLY, J)
         gather(xg_last, 3, EARLY, J)
-        for t in tiles:
-            project(t, 0)
-        add_bias(0, 0)
-        add_bias(1, 0)
-        late = held("late", [P, 4, CHUNK, PACK], BF16, slot="w_x0")
-        for n, key in enumerate((("cq", 2), ("cq", 3), ("x", 2), ("x", 3))):
-            grouped[key] = late[:, n, :, :]
+        grouped["cq", 2] = tile_of("g_cq2", 4096)
         interleave(grouped["cq", 2], c_raw[2][:])
-        interleave(grouped["cq", 3], c_raw[3][:])
-        interleave_x(xg, 2)
-        interleave_x(xg_last, 3)
-        scatter(0, 0)
-        scatter(1, 0)
+        for t in tiles:
+            project(t, 0, ("cq", "cr", "x"))
+        add_bias(0, 0)
         quantize("cq", 2)
+        scatter(0, 0)
+        for s in (4, 5):
+            decode(s)
+            negate(s)
+        grouped["cq", 3] = tile_of("g_cq3", 8192)
+        interleave(grouped["cq", 3], c_raw[3][:])
+        add_bias(1, 0, slot="s_x0")
         quantize("cq", 3)
-        quantize("x", 2)
-        quantize("x", 3)
-        add_bias(2, 0, slot="w_x0")
-        residual(2, 0)
-        residual(2, 1)
-        residual(3, 0)
+        scatter(1, 0)
+        late = shared("late", [P, 2, CHUNK, PACK], BF16, 10240)
+        grouped["x", 2], grouped["x", 3] = late[:, 0, :, :], late[:, 1, :, :]
+        for s in (4, 5):
+            subtract(s)
+            round_left(s)
+            turn_back(s)
+        regroup(2)
+        add_bias(2, 0, slot="left_bf5")
+        interleave_x(xg, 2)
+        for s in (6, 7):
+            decode(s)
+            negate(s)
+        interleave_x(xg_last, 3)
         quantize("cr", 2)
-        add_bias(3, 0, slot="g_cr2")
-        residual(3, 1)
+        quantize("x", 2)
         scatter(2, 0)
+        for s in (6, 7):
+            subtract(s)
+            round_left(s)
+            turn_back(s)
+        regroup(3)
+        add_bias(3, 0, slot="left_bf7")
+        quantize("x", 3)
         quantize("cr", 3)
         scatter(3, 0)
         for t in tiles:
-            project(t, 1)
+            project(t, 1, ("cr", "cq", "x"))
             add_bias(t, 1)
         for t in tiles:
             scatter(t, 1)

@@ -61,15 +61,17 @@ def tile_list_scatb_kernel(
         wt_s = held("wt_s", [P, N], U8)
         wx_s = held("wx_s", [P, N], U8)
         bias = held("bias", [P, N // P], F32)
-        win = {t: held(f"win{t}", [P, T], F32) for t in (0, 1)}
+        win = {t: held(f"win{t}", [P, T], F32) for t in (0, 1, 2)}
         eye = held("eye", [P, P], F32)
         sel = held("sel", [P, P * PACK], BF16)
-        sel_w = held("sel_w", [P, PACK, P], U32)
+        sel_w = [held(f"sel_w{i}", [P, P], U32) for i in range(PACK)]
         sel_s = held("sel_s", [P, P], U8)
         names = ("x", "cq", "cr")
-        own = (("cq", 0), ("cq", 1), ("cr", 0), ("x", 1), ("cr", 2), ("cr", 3))
+        own = (("cq", 0), ("cq", 1), ("cr", 0), ("cr", 1), ("cr", 2), ("cr", 3))
         grouped = {(o, q): held(f"g_{o}{q}", [P, CHUNK, PACK], BF16)[:] for o, q in own}
-        words = {(o, h): held(f"w_{o}{h}", [P, HALF], U32) for o in names for h in halves if (o, h) != ("x", 0)}
+        eye_w = held("eye_w", [P, P], U32)
+        apart = (("x", 0), ("cq", 0))
+        words = {(o, h): held(f"w_{o}{h}", [P, HALF], U32) for o in names for h in halves if (o, h) not in apart}
         words["x", 0] = shared("w_x0", [P, HALF], U32, 9216)
         scales = {(o, h): held(f"s_{o}{h}", [P, HALF], U8) for o in names for h in halves}
         ys, acc, dq, neg, left, left_bf, back = {}, {}, {}, {}, {}, {}, {}
@@ -87,7 +89,8 @@ def tile_list_scatb_kernel(
                     in_=src[0, 4 * quad : 4 * quad + 4, :].bitcast(I32),
                 )
 
-        nc.gpsimd.memset(sel[:], 0.0)
+        nc.gpsimd.memset(wx_s[:].bitcast(I32), 0)
+        nc.gpsimd.memset(sel[:].bitcast(I32), 0)
         nc.gpsimd.affine_select(
             out=sel[:],
             in_=sel[:],
@@ -97,9 +100,10 @@ def tile_list_scatb_kernel(
             base=0,
             channel_multiplier=-PACK,
         )
+        for i in range(PACK):
+            nc.gpsimd.memset(sel_w[i][:], 0)
+        nc.gpsimd.memset(wt_s[:].bitcast(I32), 0)
         make_identity(nc, eye[:])
-        nc.vector.memset(wx_s[:].bitcast(I32), 0)
-        nc.vector.memset(wt_s[:].bitcast(I32), 0)
         load_c(0)
         load_c(1)
         nc.sync.dma_start(picks[:], offs)
@@ -119,15 +123,15 @@ def tile_list_scatb_kernel(
         load_c(3)
         nc.sync.dma_start(out=wgo_sb[1][:], in_=wgo[:, HALF:J])
 
-        nc.vector.memset(sel_w[:, 1:PACK, :], 0)
         nc.vector.quantize_mx(
-            out=sel_w[:, 0, :].bitcast(FP8X4), scales=sel_s[:], in_=sel[:]
+            out=eye_w[:].bitcast(FP8X4), scales=sel_s[:], in_=sel[:]
         )
-        for i in range(1, PACK):
+        for i in range(PACK):
             nc.vector.tensor_copy(
-                out=sel_w[:, i, :].bitcast(U8)[:, i::PACK], in_=sel_w[:, 0, :].bitcast(U8)[:, 0::PACK]
+                out=sel_w[i][:].bitcast(U8)[:, i::PACK], in_=eye_w[:].bitcast(U8)[:, 0::PACK]
             )
-        for t in range(2):
+        words["cq", 0] = held("w_cq0", [P, HALF], U32, slot="eye_w")
+        for t in range(3):
             nc.vector.memset(win[t][:], 0.0)
 
         def chunk_cols(q):
@@ -154,7 +158,7 @@ def tile_list_scatb_kernel(
             for i in range(PACK):
                 nc.tensor.matmul_mx(
                     out=dq[s][:, i, :],
-                    lhsT=sel_w[:, i, :].bitcast(FP8X4),
+                    lhsT=sel_w[i][:].bitcast(FP8X4),
                     lhsT_scale=sel_s[:],
                     rhs=words["cq", h][:, lo : lo + STRIP].bitcast(FP8X4),
                     rhs_scale=scales["cq", h][:, lo : lo + STRIP],
@@ -187,7 +191,7 @@ def tile_list_scatb_kernel(
 
         def round_left(s):
             shape = [STRIP, 2, P, 2]
-            left_bf[s] = held(f"left_bf{s}", shape, BF16)
+            left_bf[s] = shared("left_bf3", shape, BF16, 1536) if s == 3 else held(f"left_bf{s}", shape, BF16)
             nc.scalar.copy(out=left_bf[s][:], in_=left[s][:].rearrange("j (u e) p -> j u p e", u=2))
 
         def turn_back(s):
@@ -198,10 +202,10 @@ def tile_list_scatb_kernel(
             for u in range(2):
                 nc.tensor.transpose(back[q][:, r, u, :], pairs[:, u * P : (u + 1) * P], eye[:])
 
-        def regroup(q):
+        def regroup(q, strips=2):
             nc.scalar.copy(
-                out=grouped["cr", q].bitcast(F32).rearrange("p (r j) u -> p r j u", r=2),
-                in_=back[q][:].rearrange("p r u j -> p r j u"),
+                out=grouped["cr", q].bitcast(F32).rearrange("p (r j) u -> p r j u", r=2)[:, 0:strips, :, :],
+                in_=back[q][:, 0:strips, :, :].rearrange("p r u j -> p r j u"),
             )
 
         def gather(xg, i, lo, hi):
@@ -250,42 +254,44 @@ def tile_list_scatb_kernel(
         def tile_of(name, offset):
             return shared(name, [P, CHUNK, PACK], BF16, offset)[:]
 
-        grouped["cr", 1] = tile_of("g_cr1", 16384 + 4 * T - 1024)
-        grouped["x", 0] = tile_of("g_x0", 3072)
         interleave(grouped["cq", 0], c_raw[0][:])
         interleave(grouped["cq", 1], c_raw[1][:])
         quantize("cq", 0)
-        decode(0)
-        decode(1)
-        subtract_on_vector(0)
+        win[3] = held("win3", [P, T], F32, slot="g_cq0")
+        nc.vector.memset(win[3][:], 0.0)
         quantize("cq", 1)
-        decode(2)
-        decode(3)
+        for s in range(4):
+            decode(s)
+        subtract_on_vector(0)
         subtract_on_vector(1)
-        subtract_on_vector(2)
-        quantize("cr", 0)
-        subtract_on_vector(3)
-        xg = held("xg", [P, PACK, EARLY], F32, slot="c_raw1")
+        negate(2)
+        negate(3)
+        for s in (2, 3):
+            subtract(s)
+            round_left(s)
+            turn_back(s)
+        regroup(1)
+        xg = held("xg", [P, PACK, EARLY], F32, slot="c_raw0")
         gather(xg, 0, 0, EARLY)
-        quantize("cr", 1)
-        for t in (2, 3):
-            win[t] = shared(f"win{t}", [P, T], F32, 16384 + (t - 2) * 4 * T)
-            nc.gpsimd.memset(win[t][:], 0.0)
+        quantize("cr", 0)
         gather(xg, 1, 0, EARLY)
         gather(xg, 2, 0, EARLY)
         gather(xg, 3, 0, CHUNK)
-        interleave_x(xg, 0)
         gather(xg, 3, CHUNK, HALF)
+        grouped["x", 0] = tile_of("g_x0", 2048)
+        grouped["x", 1] = tile_of("g_x1", 0)
+        interleave_x(xg, 0)
         interleave_x(xg, 1)
         gather(xg, 3, HALF, EARLY)
+        quantize("cr", 1)
         quantize("x", 0)
-        xg_last = shared("xg_last", [P, PACK, J - EARLY], F32, 0)
+        xg_last = shared("xg_last", [P, PACK, J - EARLY], F32, 3072)
         gather(xg_last, 0, EARLY, J)
         gather(xg_last, 1, EARLY, J)
         quantize("x", 1)
         gather(xg_last, 2, EARLY, J)
         gather(xg_last, 3, EARLY, J)
-        grouped["cq", 2] = tile_of("g_cq2", 4096)
+        grouped["cq", 2] = tile_of("g_cq2", 0)
         interleave(grouped["cq", 2], c_raw[2][:])
         for t in tiles:
             project(t, 0, ("cq", "cr", "x"))
@@ -309,19 +315,19 @@ def tile_list_scatb_kernel(
         regroup(2)
         add_bias(2, 0, slot="left_bf5")
         interleave_x(xg, 2)
-        for s in (6, 7):
-            decode(s)
-            negate(s)
+        decode(6)
+        decode(7)
+        negate(6)
+        subtract_on_vector(7)
         interleave_x(xg_last, 3)
         quantize("cr", 2)
         quantize("x", 2)
         scatter(2, 0)
-        for s in (6, 7):
-            subtract(s)
-            round_left(s)
-            turn_back(s)
-        regroup(3)
-        add_bias(3, 0, slot="left_bf7")
+        subtract(6)
+        round_left(6)
+        turn_back(6)
+        regroup(3, strips=1)
+        add_bias(3, 0, slot="left_bf6")
         quantize("x", 3)
         quantize("cr", 3)
         scatter(3, 0)

@@ -72,7 +72,7 @@ def tile_list_scatb_kernel(
         eye_w = held("eye_w", [P, P], U32)
         apart = (("x", 0), ("cq", 0))
         words = {(o, h): held(f"w_{o}{h}", [P, HALF], U32) for o in names for h in halves if (o, h) not in apart}
-        words["x", 0] = shared("w_x0", [P, HALF], U32, 9216)
+        words["x", 0] = shared("w_x0", [P, HALF], U32, 1024)
         scales = {(o, h): held(f"s_{o}{h}", [P, HALF], U8) for o in names for h in halves}
         ys, acc, dq, neg, left, left_bf, back = {}, {}, {}, {}, {}, {}, {}
 
@@ -191,7 +191,7 @@ def tile_list_scatb_kernel(
 
         def round_left(s):
             shape = [STRIP, 2, P, 2]
-            left_bf[s] = shared("left_bf3", shape, BF16, 1536) if s == 3 else held(f"left_bf{s}", shape, BF16)
+            left_bf[s] = held(f"left_bf{s}", shape, BF16)
             nc.scalar.copy(out=left_bf[s][:], in_=left[s][:].rearrange("j (u e) p -> j u p e", u=2))
 
         def turn_back(s):
@@ -239,8 +239,9 @@ def tile_list_scatb_kernel(
                     stop=(o == order[-1]),
                 )
 
-        def add_bias(t, h, slot=None):
-            ys[t, h] = held(f"ys{t}_{h}", [P, HALF], F32, slot=slot)
+        def add_bias(t, h, slot=None, offset=None):
+            name = f"ys{t}_{h}"
+            ys[t, h] = held(name, [P, HALF], F32, slot=slot) if offset is None else shared(name, [P, HALF], F32, offset)
             nc.scalar.activation(out=ys[t, h][:], in_=acc[t, h][:], func=IDENT, bias=bias[:, t : t + 1], scale=1.0)
 
         def scatter(t, h):
@@ -278,20 +279,21 @@ def tile_list_scatb_kernel(
         gather(xg, 2, 0, EARLY)
         gather(xg, 3, 0, CHUNK)
         gather(xg, 3, CHUNK, HALF)
-        grouped["x", 0] = tile_of("g_x0", 2048)
-        grouped["x", 1] = tile_of("g_x1", 0)
+        xg_last = held("xg_last", [P, PACK, J - EARLY], F32, slot="left_bf3")
+        for q in (0, 1):
+            planes = xg_last[:, 2 * q : 2 * q + 2, :].rearrange("p i j -> p (i j)")
+            grouped["x", q] = planes.bitcast(BF16).rearrange("p (j t) -> p j t", t=PACK)
         interleave_x(xg, 0)
         interleave_x(xg, 1)
         gather(xg, 3, HALF, EARLY)
         quantize("cr", 1)
         quantize("x", 0)
-        xg_last = shared("xg_last", [P, PACK, J - EARLY], F32, 3072)
         gather(xg_last, 0, EARLY, J)
         gather(xg_last, 1, EARLY, J)
         quantize("x", 1)
         gather(xg_last, 2, EARLY, J)
         gather(xg_last, 3, EARLY, J)
-        grouped["cq", 2] = tile_of("g_cq2", 0)
+        grouped["cq", 2] = held("g_cq2", [P, CHUNK, PACK], BF16, slot="x_pl0")[:]
         interleave(grouped["cq", 2], c_raw[2][:])
         for t in tiles:
             project(t, 0, ("cq", "cr", "x"))
@@ -301,19 +303,20 @@ def tile_list_scatb_kernel(
         for s in (4, 5):
             decode(s)
             negate(s)
-        grouped["cq", 3] = tile_of("g_cq3", 8192)
+        grouped["cq", 3] = tile_of("g_cq3", 0)
         interleave(grouped["cq", 3], c_raw[3][:])
         add_bias(1, 0, slot="s_x0")
         quantize("cq", 3)
+        add_bias(2, 0, offset=0)
         scatter(1, 0)
-        late = shared("late", [P, 2, CHUNK, PACK], BF16, 10240)
+        scatter(2, 0)
+        late = shared("late", [P, 2, CHUNK, PACK], BF16, 2048)
         grouped["x", 2], grouped["x", 3] = late[:, 0, :, :], late[:, 1, :, :]
         for s in (4, 5):
             subtract(s)
             round_left(s)
             turn_back(s)
         regroup(2)
-        add_bias(2, 0, slot="left_bf5")
         interleave_x(xg, 2)
         decode(6)
         decode(7)
@@ -322,7 +325,6 @@ def tile_list_scatb_kernel(
         interleave_x(xg_last, 3)
         quantize("cr", 2)
         quantize("x", 2)
-        scatter(2, 0)
         subtract(6)
         round_left(6)
         turn_back(6)

@@ -1,7 +1,6 @@
 from contextlib import ExitStack
 
 import concourse.mybir as mybir
-from concourse.masks import make_identity
 
 K, L, N, T, J = 512, 512, 512, 2048, 1024
 FLOPS = 4 * 2 * 512 * 512 * 1024
@@ -24,8 +23,6 @@ PACK = 4
 HALF = 512
 CHUNK = 256
 STRIP = 128
-EARLY = 768
-LIST_COLS = HALF // 16
 
 
 def tile_list_scatb_kernel(
@@ -35,15 +32,11 @@ def tile_list_scatb_kernel(
     with ExitStack() as ctx:
         lists = ctx.enter_context(tc.tile_pool(name="lists", bufs=1))
         keep = ctx.enter_context(tc.tile_pool(name="keep", bufs=1))
-        over = ctx.enter_context(tc.tile_pool(name="over", bufs=1))
         ps_dq = ctx.enter_context(tc.psum_pool(name="ps_dq", bufs=4))
         ps_y = ctx.enter_context(tc.psum_pool(name="ps_y", bufs=4))
 
         def held(name, shape, dtype, slot=None):
             return keep.tile(shape, dtype, name=name, tag=slot or name, align_bytes=64)
-
-        def shared(name, shape, dtype, offset):
-            return over.tile(shape, dtype, name=name, align_bytes=64, offset=offset)
 
         picks = lists.tile([P, J // 16], U16, name="picks")
         places = lists.tile([P, J // 16], U16, name="places")
@@ -53,28 +46,22 @@ def tile_list_scatb_kernel(
 
         x_pl = [held(f"x_pl{i}", [P, T], F32) for i in range(PACK)]
         c_raw = [held(f"c_raw{q}", [P, PACK, CHUNK], F32) for q in chunks]
-        wgt_a = held("wgt_a", [P, EARLY], F32)
-        wgt_b = held("wgt_b", [P, J - EARLY], F32)
+        wgt_sb = held("wgt_sb", [P, J], F32)
         wgo_sb = [held(f"wgo_sb{h}", [P, HALF], F32) for h in halves]
         wt_w = held("wt_w", [P, 2 * N], U8)
         wx_w = held("wx_w", [P, N], U32)
-        wt_s = held("wt_s", [P, N], U8)
-        wx_s = held("wx_s", [P, N], U8)
+        w_s = held("w_s", [P, 2 * N], U8)
         bias = held("bias", [P, N // P], F32)
-        win = {t: held(f"win{t}", [P, T], F32) for t in (0, 1, 2)}
+        win = [held(f"win{t}", [P, T], F32) for t in tiles]
+        ones = held("ones", [P, PACK * P + PACK], BF16)
         eye = held("eye", [P, P], F32)
-        sel = held("sel", [P, P * PACK], BF16)
-        sel_w = [held(f"sel_w{i}", [P, P], U32) for i in range(PACK)]
-        sel_s = held("sel_s", [P, P], U8)
+        sel = held("sel", [P, PACK, PACK * P], BF16)
+        sel_w = held("sel_w", [P, PACK * P], U32)
+        sel_s = held("sel_s", [P, PACK * P], U8)
         names = ("x", "cq", "cr")
-        own = (("cq", 0), ("cq", 1), ("cr", 0), ("cr", 1), ("cr", 2), ("cr", 3))
-        grouped = {(o, q): held(f"g_{o}{q}", [P, CHUNK, PACK], BF16)[:] for o, q in own}
-        eye_w = held("eye_w", [P, P], U32)
-        apart = (("x", 0), ("cq", 0))
-        words = {(o, h): held(f"w_{o}{h}", [P, HALF], U32) for o in names for h in halves if (o, h) not in apart}
-        words["x", 0] = shared("w_x0", [P, HALF], U32, 1024)
+        words = {(o, h): held(f"w_{o}{h}", [P, HALF], U32) for o in names for h in halves}
         scales = {(o, h): held(f"s_{o}{h}", [P, HALF], U8) for o in names for h in halves}
-        ys, acc, dq, neg, left, left_bf, back = {}, {}, {}, {}, {}, {}, {}
+        grouped, ys, acc, dq, neg, left, left_bf, back = {}, {}, {}, {}, {}, {}, {}, {}
 
         x_src = xT.rearrange("(p i) t -> i p t", i=PACK)
         c_src = c.rearrange("(p i) j -> p i j", i=PACK)
@@ -82,75 +69,74 @@ def tile_list_scatb_kernel(
         def load_c(q):
             nc.sync.dma_start(out=c_raw[q][:], in_=c_src[:, :, q * CHUNK : (q + 1) * CHUNK])
 
-        def load_scales(plane, src):
-            for quad in range(4):
-                nc.sync.dma_start(
-                    out=plane[32 * quad : 32 * quad + 4, :].bitcast(I32),
-                    in_=src[0, 4 * quad : 4 * quad + 4, :].bitcast(I32),
-                )
+        def load_x(i):
+            nc.sync.dma_start(out=x_pl[i][:], in_=x_src[i])
 
-        nc.gpsimd.memset(wx_s[:].bitcast(I32), 0)
-        nc.gpsimd.memset(sel[:].bitcast(I32), 0)
+        def load_scales(n):
+            which, quad = divmod(n, 4)
+            src = (wx_scales, wt_scales)[which]
+            nc.sync.dma_start(
+                out=w_s[32 * quad : 32 * quad + 4, which * N : (which + 1) * N].bitcast(I32),
+                in_=src[0, 4 * quad : 4 * quad + 4, :].bitcast(I32),
+            )
+
+        nc.gpsimd.memset(ones[:].bitcast(I32), 0)
         nc.gpsimd.affine_select(
-            out=sel[:],
-            in_=sel[:],
-            pattern=[[1, PACK * P]],
+            out=ones[:],
+            in_=ones[:],
+            pattern=[[1, PACK * P + PACK]],
             compare_op=mybir.AluOpType.not_equal,
             fill=1.0,
-            base=0,
+            base=-(PACK - 1),
             channel_multiplier=-PACK,
         )
-        for i in range(PACK):
-            nc.gpsimd.memset(sel_w[i][:], 0)
-        nc.gpsimd.memset(wt_s[:].bitcast(I32), 0)
-        make_identity(nc, eye[:])
+        nc.gpsimd.memset(w_s[:].bitcast(I32), 0)
+
+        nc.sync.dma_start(picks[:], offs)
         load_c(0)
         load_c(1)
-        nc.sync.dma_start(picks[:], offs)
-        nc.sync.dma_start(out=wgt_a[:], in_=wgt[:, 0:EARLY])
-        load_scales(wx_s, wx_scales)
-        for i in range(PACK):
-            nc.sync.dma_start(out=x_pl[i][:], in_=x_src[i])
-        load_scales(wt_s, wt_scales)
-        nc.sync.dma_start(out=wgt_b[:], in_=wgt[:, EARLY:J])
-        nc.sync.dma_start(out=wx_w[:].bitcast(I32), in_=wx_words[0].rearrange("p n t -> p (n t)").bitcast(I32))
-        nc.sync.dma_start(out=wt_w[:].bitcast(I32), in_=wt_words[0].bitcast(I32))
-        load_c(2)
+        nc.sync.dma_start(out=wgt_sb[:], in_=wgt)
+        load_x(0)
+        for n in (0, 1, 2):
+            load_scales(n)
+        load_x(1)
+        load_scales(3)
+        load_scales(4)
+        load_x(2)
+        for n in (5, 6, 7):
+            load_scales(n)
         with nc.allow_non_contiguous_dma(reason="one bias value a partition"):
             nc.sync.dma_start(out=bias[:], in_=b.rearrange("(t p) -> p t", p=P))
-        nc.sync.dma_start(out=wgo_sb[0][:], in_=wgo[:, 0:HALF])
         nc.sync.dma_start(places[:], offs2)
+        load_x(3)
+        nc.sync.dma_start(out=wt_w[:].bitcast(I32), in_=wt_words[0].bitcast(I32))
+        nc.sync.dma_start(out=wx_w[:].bitcast(I32), in_=wx_words[0].rearrange("p n t -> p (n t)").bitcast(I32))
+        nc.sync.dma_start(out=wgo_sb[0][:], in_=wgo[:, 0:HALF])
+        load_c(2)
         load_c(3)
         nc.sync.dma_start(out=wgo_sb[1][:], in_=wgo[:, HALF:J])
 
-        nc.vector.quantize_mx(
-            out=eye_w[:].bitcast(FP8X4), scales=sel_s[:], in_=sel[:]
-        )
-        for i in range(PACK):
-            nc.vector.tensor_copy(
-                out=sel_w[i][:].bitcast(U8)[:, i::PACK], in_=eye_w[:].bitcast(U8)[:, 0::PACK]
-            )
-        words["cq", 0] = held("w_cq0", [P, HALF], U32, slot="eye_w")
-        for t in range(3):
-            nc.vector.memset(win[t][:], 0.0)
-
-        def chunk_cols(q):
-            lo = q * CHUNK % HALF
-            return q * CHUNK // HALF, slice(lo, lo + CHUNK)
-
-        def interleave(dst, src):
+        def interleave(o, lo, hi, src, slot=None):
+            grouped[o, lo] = held(f"g_{o}{lo}", [P, hi - lo, PACK], BF16, slot=slot)
             nc.scalar.copy(
-                out=dst.rearrange("p (a e) t -> p a t e", e=4),
+                out=grouped[o, lo][:].rearrange("p (a e) t -> p a t e", e=4),
                 in_=src.rearrange("p t (a e) -> p a t e", e=4),
             )
 
-        def quantize(o, q):
-            h, cols = chunk_cols(q)
+        def quantize(o, lo, hi):
+            h, at = divmod(lo, HALF)
+            cols = slice(at, at + hi - lo)
             nc.vector.quantize_mx(
                 out=words[o, h][:, cols].bitcast(FP8X4),
                 scales=scales[o, h][:, cols],
-                in_=grouped[o, q].rearrange("p j t -> p (j t)"),
+                in_=grouped[o, lo][:].rearrange("p j t -> p (j t)"),
             )
+
+        def interleave_c(q):
+            interleave("cq", q * CHUNK, (q + 1) * CHUNK, c_raw[q][:])
+
+        def quantize_chunk(o, q):
+            quantize(o, q * CHUNK, (q + 1) * CHUNK)
 
         def decode(s):
             h, lo = divmod(s * STRIP, HALF)
@@ -158,25 +144,29 @@ def tile_list_scatb_kernel(
             for i in range(PACK):
                 nc.tensor.matmul_mx(
                     out=dq[s][:, i, :],
-                    lhsT=sel_w[i][:].bitcast(FP8X4),
-                    lhsT_scale=sel_s[:],
+                    lhsT=sel_w[:, i * P : (i + 1) * P].bitcast(FP8X4),
+                    lhsT_scale=sel_s[:, i * P : (i + 1) * P],
                     rhs=words["cq", h][:, lo : lo + STRIP].bitcast(FP8X4),
                     rhs_scale=scales["cq", h][:, lo : lo + STRIP],
                     start=True,
                     stop=True,
                 )
 
-        def subtract_on_vector(s):
+        def residual_tile(q):
+            grouped["cr", q * CHUNK] = held(f"g_cr{q}", [P, CHUNK, PACK], BF16)
+            return grouped["cr", q * CHUNK]
+
+        def subtract_on_vector(s, dst):
             q, lo = divmod(s * STRIP, CHUNK)
             nc.vector.tensor_tensor(
-                out=grouped["cr", q][:, lo : lo + STRIP, :].rearrange("p (a e) t -> p a t e", e=4),
+                out=dst[:, lo : lo + STRIP, :].rearrange("p (a e) t -> p a t e", e=4),
                 in0=c_raw[q][:, :, lo : lo + STRIP].rearrange("p t (a e) -> p a t e", e=4),
                 in1=dq[s][:].rearrange("p t (a e) -> p a t e", e=4),
                 op=SUB,
             )
 
         def negate(s):
-            neg[s] = held(f"neg{s}", [P, PACK, STRIP], F32)
+            neg[s] = held(f"neg{s}", [P, PACK, STRIP], F32, slot=f"neg{s % 2}")
             nc.scalar.activation(out=neg[s][:], in_=dq[s][:], func=COPY, scale=-1.0)
 
         def subtract(s):
@@ -190,8 +180,7 @@ def tile_list_scatb_kernel(
                     )
 
         def round_left(s):
-            shape = [STRIP, 2, P, 2]
-            left_bf[s] = held(f"left_bf{s}", shape, BF16)
+            left_bf[s] = held(f"left_bf{s}", [STRIP, 2, P, 2], BF16)
             nc.scalar.copy(out=left_bf[s][:], in_=left[s][:].rearrange("j (u e) p -> j u p e", u=2))
 
         def turn_back(s):
@@ -202,140 +191,150 @@ def tile_list_scatb_kernel(
             for u in range(2):
                 nc.tensor.transpose(back[q][:, r, u, :], pairs[:, u * P : (u + 1) * P], eye[:])
 
-        def regroup(q, strips=2):
+        def regroup(q):
             nc.scalar.copy(
-                out=grouped["cr", q].bitcast(F32).rearrange("p (r j) u -> p r j u", r=2)[:, 0:strips, :, :],
-                in_=back[q][:, 0:strips, :, :].rearrange("p r u j -> p r j u"),
+                out=residual_tile(q)[:].bitcast(F32).rearrange("p (r j) u -> p r j u", r=2),
+                in_=back[q][:].rearrange("p r u j -> p r j u"),
             )
 
-        def gather(xg, i, lo, hi):
-            base, factors = (0, wgt_a) if hi <= EARLY else (EARLY, wgt_b)
-            nc.vector.tensor_tensor(
-                xg[:, i, lo - base : hi - base],
-                x_pl[i][:].indirect(picks[:, lo // 16 : hi // 16]),
-                factors[:, lo - base : hi - base],
-                MULT,
-            )
+        def decode_and_negate(q):
+            for s in (2 * q, 2 * q + 1):
+                decode(s)
+            for s in (2 * q, 2 * q + 1):
+                negate(s)
+                subtract(s)
 
-        def interleave_x(xg, q):
-            lo = q * CHUNK % EARLY
-            interleave(grouped["x", q], xg[:, :, lo : lo + CHUNK])
+        def round_and_turn(q):
+            for s in (2 * q, 2 * q + 1):
+                round_left(s)
+                turn_back(s)
 
-        def project(t, h, order):
-            acc[t, h] = ps_y.tile([P, HALF], F32, name="acc")
+        def project(t, lo, hi):
+            acc[t, lo] = ps_y.tile([P, hi - lo], F32, name="acc", tag="acc")
             ncols = slice(t * P, (t + 1) * P)
-            for o in order:
-                if o == "x":
-                    w, ws = wt_w[:, 2 * t * P : 2 * (t + 1) * P].bitcast(FP4X4), wt_s[:, ncols]
-                else:
-                    w, ws = wx_w[:, ncols].bitcast(FP8X4), wx_s[:, ncols]
-                nc.tensor.matmul_mx(
-                    out=acc[t, h][:],
-                    lhsT=w,
-                    lhsT_scale=ws,
-                    rhs=words[o, h][:].bitcast(FP8X4),
-                    rhs_scale=scales[o, h][:],
-                    start=(o == order[0]),
-                    stop=(o == order[-1]),
-                )
+            order = ("cr", "cq", "x") if lo >= HALF else ("cq", "cr", "x")
+            step = HALF if hi - lo == HALF else STRIP
+            for at in range(lo, hi, step):
+                h, first = divmod(at, HALF)
+                cols = slice(first, first + step)
+                for o in order:
+                    if o == "x":
+                        w, ws = wt_w[:, 2 * t * P : 2 * (t + 1) * P].bitcast(FP4X4), w_s[:, N + t * P : N + (t + 1) * P]
+                    else:
+                        w, ws = wx_w[:, ncols].bitcast(FP8X4), w_s[:, ncols]
+                    nc.tensor.matmul_mx(
+                        out=acc[t, lo][:, at - lo : at - lo + step],
+                        lhsT=w,
+                        lhsT_scale=ws,
+                        rhs=words[o, h][:, cols].bitcast(FP8X4),
+                        rhs_scale=scales[o, h][:, cols],
+                        start=(o == order[0]),
+                        stop=(o == order[-1]),
+                    )
 
-        def add_bias(t, h, slot=None, offset=None):
-            name = f"ys{t}_{h}"
-            ys[t, h] = held(name, [P, HALF], F32, slot=slot) if offset is None else shared(name, [P, HALF], F32, offset)
-            nc.scalar.activation(out=ys[t, h][:], in_=acc[t, h][:], func=IDENT, bias=bias[:, t : t + 1], scale=1.0)
-
-        def scatter(t, h):
+        def finish(t, lo, hi, slot=None):
+            ys[t, lo] = held(f"ys{t}_{lo}", [P, hi - lo], F32, slot=slot)
+            nc.scalar.activation(out=ys[t, lo][:], in_=acc[t, lo][:], func=IDENT, bias=bias[:, t : t + 1], scale=1.0)
+            h, at = divmod(lo, HALF)
             nc.vector.tensor_tensor(
-                win[t][:].indirect(places[:, h * LIST_COLS : (h + 1) * LIST_COLS]),
-                ys[t, h][:],
-                wgo_sb[h][:],
+                win[t][:].indirect(places[:, lo // 16 : hi // 16]),
+                ys[t, lo][:],
+                wgo_sb[h][:, at : at + hi - lo],
+                MULT,
+            )
+            if hi == J:
+                nc.sync.dma_start(out=out[t * P : (t + 1) * P, :], in_=win[t][:])
+
+        for i in range(PACK):
+            nc.scalar.copy(out=sel[:, i, :], in_=ones[:, PACK - 1 - i : PACK - 1 - i + PACK * P])
+        nc.vector.memset(win[0][:], 0.0)
+        nc.vector.memset(win[1][:], 0.0)
+        nc.vector.quantize_mx(out=sel_w[:].bitcast(FP8X4), scales=sel_s[:], in_=sel[:].rearrange("p i m -> p (i m)"))
+        nc.vector.memset(win[2][:], 0.0)
+        interleave_c(0)
+        interleave_c(1)
+        nc.scalar.copy(out=eye[:], in_=ones[:, PACK - 1 : PACK * P : PACK])
+        quantize_chunk("cq", 0)
+        nc.vector.memset(win[3][:], 0.0)
+        quantize_chunk("cq", 1)
+        decode(0)
+        decode(1)
+        first_left = residual_tile(0)
+        subtract_on_vector(0, first_left)
+        subtract_on_vector(1, first_left)
+        quantize_chunk("cr", 0)
+        decode_and_negate(1)
+        round_and_turn(1)
+        regroup(1)
+
+        xg = held("xg", [P, 2 * PACK * HALF - STRIP], F32, slot="c_raw0")
+        xg_half = {
+            0: xg[:, PACK * HALF - STRIP : 2 * PACK * HALF - STRIP].rearrange("p (i j) -> p i j", i=PACK),
+            1: xg[:, 0 : PACK * HALF].rearrange("p (i j) -> p i j", i=PACK),
+        }
+
+        def gather(i, lo, hi):
+            h, at = divmod(lo, HALF)
+            nc.vector.tensor_tensor(
+                xg_half[h][:, i, at : at + hi - lo],
+                x_pl[i][:].indirect(picks[:, lo // 16 : hi // 16]),
+                wgt_sb[:, lo:hi],
                 MULT,
             )
 
-        def tile_of(name, offset):
-            return shared(name, [P, CHUNK, PACK], BF16, offset)[:]
+        def interleave_x(lo, hi, slot=None):
+            h, at = divmod(lo, HALF)
+            interleave("x", lo, hi, xg_half[h][:, :, at : at + hi - lo], slot=slot)
 
-        interleave(grouped["cq", 0], c_raw[0][:])
-        interleave(grouped["cq", 1], c_raw[1][:])
-        quantize("cq", 0)
-        win[3] = held("win3", [P, T], F32, slot="g_cq0")
-        nc.vector.memset(win[3][:], 0.0)
-        quantize("cq", 1)
-        for s in range(4):
-            decode(s)
-        subtract_on_vector(0)
-        subtract_on_vector(1)
-        negate(2)
-        negate(3)
-        for s in (2, 3):
-            subtract(s)
-            round_left(s)
-            turn_back(s)
-        regroup(1)
-        xg = held("xg", [P, PACK, EARLY], F32, slot="c_raw0")
-        gather(xg, 0, 0, EARLY)
-        quantize("cr", 0)
-        gather(xg, 1, 0, EARLY)
-        gather(xg, 2, 0, EARLY)
-        gather(xg, 3, 0, CHUNK)
-        gather(xg, 3, CHUNK, HALF)
-        xg_last = held("xg_last", [P, PACK, J - EARLY], F32, slot="left_bf3")
-        for q in (0, 1):
-            planes = xg_last[:, 2 * q : 2 * q + 2, :].rearrange("p i j -> p (i j)")
-            grouped["x", q] = planes.bitcast(BF16).rearrange("p (j t) -> p j t", t=PACK)
-        interleave_x(xg, 0)
-        interleave_x(xg, 1)
-        gather(xg, 3, HALF, EARLY)
-        quantize("cr", 1)
-        quantize("x", 0)
-        gather(xg_last, 0, EARLY, J)
-        gather(xg_last, 1, EARLY, J)
-        quantize("x", 1)
-        gather(xg_last, 2, EARLY, J)
-        gather(xg_last, 3, EARLY, J)
-        grouped["cq", 2] = held("g_cq2", [P, CHUNK, PACK], BF16, slot="x_pl0")[:]
-        interleave(grouped["cq", 2], c_raw[2][:])
+        for i in range(PACK - 1):
+            gather(i, 0, HALF)
+            gather(i, HALF, J)
+        quantize_chunk("cr", 1)
+        last = PACK - 1
+        gather(last, 0, STRIP)
+        gather(last, STRIP, HALF)
+        interleave_x(0, STRIP)
+        quantize("x", 0, STRIP)
+        gather(last, HALF, J)
+        interleave_x(STRIP, CHUNK)
+        quantize("x", STRIP, CHUNK)
         for t in tiles:
-            project(t, 0, ("cq", "cr", "x"))
-        add_bias(0, 0)
-        quantize("cq", 2)
-        scatter(0, 0)
-        for s in (4, 5):
-            decode(s)
-            negate(s)
-        grouped["cq", 3] = tile_of("g_cq3", 0)
-        interleave(grouped["cq", 3], c_raw[3][:])
-        add_bias(1, 0, slot="s_x0")
-        quantize("cq", 3)
-        add_bias(2, 0, offset=0)
-        scatter(1, 0)
-        scatter(2, 0)
-        late = shared("late", [P, 2, CHUNK, PACK], BF16, 2048)
-        grouped["x", 2], grouped["x", 3] = late[:, 0, :, :], late[:, 1, :, :]
-        for s in (4, 5):
-            subtract(s)
-            round_left(s)
-            turn_back(s)
+            project(t, 0, STRIP)
+        finish(0, 0, STRIP)
+        finish(1, 0, STRIP)
+        interleave_x(CHUNK, HALF, slot=f"g_x{STRIP}")
+        quantize("x", CHUNK, HALF)
+        finish(2, 0, STRIP)
+        finish(3, 0, STRIP)
+        for t in tiles:
+            project(t, STRIP, HALF)
+        interleave_c(2)
+        quantize_chunk("cq", 2)
+        finish(0, STRIP, HALF)
+        interleave_c(3)
+        quantize_chunk("cq", 3)
+        finish(1, STRIP, HALF)
+        decode_and_negate(2)
+        interleave_x(2 * CHUNK, 3 * CHUNK, slot=f"g_cq{2 * CHUNK}")
+        quantize_chunk("x", 2)
+        round_and_turn(2)
+        finish(2, STRIP, HALF)
+        decode_and_negate(3)
         regroup(2)
-        interleave_x(xg, 2)
-        decode(6)
-        decode(7)
-        negate(6)
-        subtract_on_vector(7)
-        interleave_x(xg_last, 3)
-        quantize("cr", 2)
-        quantize("x", 2)
-        subtract(6)
-        round_left(6)
-        turn_back(6)
-        regroup(3, strips=1)
-        add_bias(3, 0, slot="left_bf6")
-        quantize("x", 3)
-        quantize("cr", 3)
-        scatter(3, 0)
-        for t in tiles:
-            project(t, 1, ("cr", "cq", "x"))
-            add_bias(t, 1)
-        for t in tiles:
-            scatter(t, 1)
-            nc.sync.dma_start(out=out[t * P : (t + 1) * P, :], in_=win[t][:])
+        quantize_chunk("cr", 2)
+        finish(3, STRIP, HALF, slot="left_bf5")
+        for t in (0, 1):
+            project(t, HALF, 3 * CHUNK)
+        interleave_x(3 * CHUNK, J, slot="left_bf4")
+        quantize_chunk("x", 3)
+        finish(0, HALF, 3 * CHUNK)
+        round_and_turn(3)
+        regroup(3)
+        quantize_chunk("cr", 3)
+        finish(1, HALF, 3 * CHUNK, slot="left_bf7")
+        for t in (0, 1):
+            project(t, 3 * CHUNK, J)
+            finish(t, 3 * CHUNK, J)
+        for t in (2, 3):
+            project(t, HALF, J)
+            finish(t, HALF, J)

@@ -14,7 +14,6 @@ U8 = mybir.dt.uint8
 FP8X4 = mybir.dt.float8_e4m3fn_x4
 FP4X4 = mybir.dt.float4_e2m1fn_x4
 MULT = mybir.AluOpType.mult
-SUB = mybir.AluOpType.subtract
 COPY = mybir.ActivationFunctionType.Copy
 IDENT = mybir.ActivationFunctionType.Identity
 
@@ -32,6 +31,7 @@ def tile_list_scatb_kernel(
     with ExitStack() as ctx:
         lists = ctx.enter_context(tc.tile_pool(name="lists", bufs=1))
         keep = ctx.enter_context(tc.tile_pool(name="keep", bufs=1))
+        over = ctx.enter_context(tc.tile_pool(name="over", bufs=1))
         ps_dq = ctx.enter_context(tc.psum_pool(name="ps_dq", bufs=4))
         ps_y = ctx.enter_context(tc.psum_pool(name="ps_y", bufs=4))
 
@@ -52,14 +52,24 @@ def tile_list_scatb_kernel(
         wx_w = held("wx_w", [P, N], U32)
         w_s = held("w_s", [P, 2 * N], U8)
         bias = held("bias", [P, N // P], F32)
+        bias_rows = held("bias_rows", [P, P], F32)
         win = [held(f"win{t}", [P, T], F32) for t in tiles]
-        ones = held("ones", [P, PACK * P + PACK], BF16)
+        ones = over.tile([P, PACK * P + PACK], BF16, name="ones", align_bytes=64, offset=1536)
         eye = held("eye", [P, P], F32)
-        sel = held("sel", [P, PACK, PACK * P], BF16)
+        sel = over.tile([P, PACK, PACK * P], BF16, name="sel", align_bytes=64, offset=4096)
         sel_w = held("sel_w", [P, PACK * P], U32)
         sel_s = held("sel_s", [P, PACK * P], U8)
         names = ("x", "cq", "cr")
-        words = {(o, h): held(f"w_{o}{h}", [P, HALF], U32) for o in names for h in halves}
+        words = {(o, h): held(f"w_{o}{h}", [P, HALF], U32) for o in names for h in halves if (o, h) != ("cr", 0)}
+        early_cr = {}
+
+        def codes(o, lo, hi):
+            if o == "cr" and lo < HALF:
+                q, at = divmod(lo, CHUNK)
+                return early_cr[q][:, at : at + hi - lo].bitcast(FP8X4)
+            h, at = divmod(lo, HALF)
+            return words[o, h][:, at : at + hi - lo].bitcast(FP8X4)
+
         scales = {(o, h): held(f"s_{o}{h}", [P, HALF], U8) for o in names for h in halves}
         grouped, ys, acc, dq, neg, left, left_bf, back = {}, {}, {}, {}, {}, {}, {}, {}
 
@@ -91,22 +101,21 @@ def tile_list_scatb_kernel(
             channel_multiplier=-PACK,
         )
         nc.gpsimd.memset(w_s[:].bitcast(I32), 0)
+        nc.gpsimd.memset(bias_rows[:], 0.0)
 
         nc.sync.dma_start(picks[:], offs)
         load_c(0)
-        load_c(1)
         nc.sync.dma_start(out=wgt_sb[:], in_=wgt)
         load_x(0)
-        for n in (0, 1, 2):
+        load_c(1)
+        for n in range(5):
             load_scales(n)
         load_x(1)
-        load_scales(3)
-        load_scales(4)
+        load_scales(5)
         load_x(2)
-        for n in (5, 6, 7):
-            load_scales(n)
-        with nc.allow_non_contiguous_dma(reason="one bias value a partition"):
-            nc.sync.dma_start(out=bias[:], in_=b.rearrange("(t p) -> p t", p=P))
+        load_scales(6)
+        load_scales(7)
+        nc.sync.dma_start(out=bias_rows[0 : N // P, :], in_=b.rearrange("(t p) -> t p", p=P))
         nc.sync.dma_start(places[:], offs2)
         load_x(3)
         nc.sync.dma_start(out=wt_w[:].bitcast(I32), in_=wt_words[0].bitcast(I32))
@@ -117,7 +126,10 @@ def tile_list_scatb_kernel(
         nc.sync.dma_start(out=wgo_sb[1][:], in_=wgo[:, HALF:J])
 
         def interleave(o, lo, hi, src, slot=None):
-            grouped[o, lo] = held(f"g_{o}{lo}", [P, hi - lo, PACK], BF16, slot=slot)
+            if o == "cq" and lo < HALF:
+                grouped[o, lo] = over.tile([P, hi - lo, PACK], BF16, name=f"g_cq{lo}", align_bytes=64, offset=2048 - 8 * lo)
+            else:
+                grouped[o, lo] = held(f"g_{o}{lo}", [P, hi - lo, PACK], BF16, slot=slot)
             nc.scalar.copy(
                 out=grouped[o, lo][:].rearrange("p (a e) t -> p a t e", e=4),
                 in_=src.rearrange("p t (a e) -> p a t e", e=4),
@@ -127,7 +139,7 @@ def tile_list_scatb_kernel(
             h, at = divmod(lo, HALF)
             cols = slice(at, at + hi - lo)
             nc.vector.quantize_mx(
-                out=words[o, h][:, cols].bitcast(FP8X4),
+                out=codes(o, lo, hi),
                 scales=scales[o, h][:, cols],
                 in_=grouped[o, lo][:].rearrange("p j t -> p (j t)"),
             )
@@ -155,15 +167,6 @@ def tile_list_scatb_kernel(
         def residual_tile(q):
             grouped["cr", q * CHUNK] = held(f"g_cr{q}", [P, CHUNK, PACK], BF16)
             return grouped["cr", q * CHUNK]
-
-        def subtract_on_vector(s, dst):
-            q, lo = divmod(s * STRIP, CHUNK)
-            nc.vector.tensor_tensor(
-                out=dst[:, lo : lo + STRIP, :].rearrange("p (a e) t -> p a t e", e=4),
-                in0=c_raw[q][:, :, lo : lo + STRIP].rearrange("p t (a e) -> p a t e", e=4),
-                in1=dq[s][:].rearrange("p t (a e) -> p a t e", e=4),
-                op=SUB,
-            )
 
         def negate(s):
             neg[s] = held(f"neg{s}", [P, PACK, STRIP], F32, slot=f"neg{s % 2}")
@@ -226,7 +229,7 @@ def tile_list_scatb_kernel(
                         out=acc[t, lo][:, at - lo : at - lo + step],
                         lhsT=w,
                         lhsT_scale=ws,
-                        rhs=words[o, h][:, cols].bitcast(FP8X4),
+                        rhs=codes(o, at, at + step),
                         rhs_scale=scales[o, h][:, cols],
                         start=(o == order[0]),
                         stop=(o == order[-1]),
@@ -245,29 +248,16 @@ def tile_list_scatb_kernel(
             if hi == J:
                 nc.sync.dma_start(out=out[t * P : (t + 1) * P, :], in_=win[t][:])
 
+        for t in tiles:
+            nc.vector.memset(win[t][:], 0.0)
         for i in range(PACK):
             nc.scalar.copy(out=sel[:, i, :], in_=ones[:, PACK - 1 - i : PACK - 1 - i + PACK * P])
-        nc.vector.memset(win[0][:], 0.0)
-        nc.vector.memset(win[1][:], 0.0)
-        nc.vector.quantize_mx(out=sel_w[:].bitcast(FP8X4), scales=sel_s[:], in_=sel[:].rearrange("p i m -> p (i m)"))
-        nc.vector.memset(win[2][:], 0.0)
-        interleave_c(0)
-        interleave_c(1)
         nc.scalar.copy(out=eye[:], in_=ones[:, PACK - 1 : PACK * P : PACK])
+        nc.vector.quantize_mx(out=sel_w[:].bitcast(FP8X4), scales=sel_s[:], in_=sel[:].rearrange("p i m -> p (i m)"))
+        interleave_c(0)
         quantize_chunk("cq", 0)
-        nc.vector.memset(win[3][:], 0.0)
-        quantize_chunk("cq", 1)
-        decode(0)
-        decode(1)
-        first_left = residual_tile(0)
-        subtract_on_vector(0, first_left)
-        subtract_on_vector(1, first_left)
-        quantize_chunk("cr", 0)
-        decode_and_negate(1)
-        round_and_turn(1)
-        regroup(1)
 
-        xg = held("xg", [P, 2 * PACK * HALF - STRIP], F32, slot="c_raw0")
+        xg = over.tile([P, 2 * PACK * HALF - STRIP], F32, name="xg", align_bytes=64, offset=2048)
         xg_half = {
             0: xg[:, PACK * HALF - STRIP : 2 * PACK * HALF - STRIP].rearrange("p (i j) -> p i j", i=PACK),
             1: xg[:, 0 : PACK * HALF].rearrange("p (i j) -> p i j", i=PACK),
@@ -286,10 +276,24 @@ def tile_list_scatb_kernel(
             h, at = divmod(lo, HALF)
             interleave("x", lo, hi, xg_half[h][:, :, at : at + hi - lo], slot=slot)
 
-        for i in range(PACK - 1):
-            gather(i, 0, HALF)
-            gather(i, HALF, J)
-        quantize_chunk("cr", 1)
+        gather(0, 0, HALF)
+        gather(0, HALF, J)
+        decode_and_negate(0)
+        interleave_c(1)
+        quantize_chunk("cq", 1)
+        round_and_turn(0)
+        decode_and_negate(1)
+        regroup(0)
+        round_and_turn(1)
+        regroup(1)
+        bias_turned = ps_dq.tile([P, P], F32, name="bias_turned", tag="bank")
+        nc.tensor.transpose(bias_turned[:], bias_rows[:], eye[:])
+        nc.scalar.copy(out=bias[:], in_=bias_turned[:, 0 : N // P])
+        for q in (0, 1):
+            gather(q + 1, 0, HALF)
+            gather(q + 1, HALF, J)
+            early_cr[q] = held(f"w_cr_early{q}", [P, CHUNK], U32, slot=f"x_pl{q + 1}")
+            quantize_chunk("cr", q)
         last = PACK - 1
         gather(last, 0, STRIP)
         gather(last, STRIP, HALF)

@@ -22,6 +22,7 @@ PACK = 4
 HALF = 512
 CHUNK = 256
 STRIP = 128
+GROUPS = 8
 
 
 def tile_list_scatb_kernel(
@@ -32,7 +33,7 @@ def tile_list_scatb_kernel(
         lists = ctx.enter_context(tc.tile_pool(name="lists", bufs=1))
         keep = ctx.enter_context(tc.tile_pool(name="keep", bufs=1))
         over = ctx.enter_context(tc.tile_pool(name="over", bufs=1))
-        ps_dq = ctx.enter_context(tc.psum_pool(name="ps_dq", bufs=4))
+        ps_dq = ctx.enter_context(tc.psum_pool(name="ps_dq", bufs=1))
         ps_y = ctx.enter_context(tc.psum_pool(name="ps_y", bufs=4))
 
         def held(name, shape, dtype, slot=None):
@@ -44,8 +45,16 @@ def tile_list_scatb_kernel(
         chunks = range(J // CHUNK)
         tiles = range(N // P)
 
-        x_pl = [held(f"x_pl{i}", [P, T], F32) for i in range(PACK)]
+        x_pl = [over.tile([P, T], F32, name="x_pl0", align_bytes=64, offset=42624)]
+        x_pl.append(over.tile([P, T], F32, name="x_pl1", align_bytes=64, offset=50816))
+        x_pl.append(held("x_pl2", [P, T], F32))
+        x_pl.append(over.tile([P, T], F32, name="x_pl3", align_bytes=64, offset=73216))
         c_raw = [held(f"c_raw{q}", [P, PACK, CHUNK], F32) for q in chunks]
+        wgt_rows = held("wgt_rows", [P, STRIP], F32)
+        wgt_wide = [
+            held("wgt_wide0", [P, PACK, GROUPS, P // GROUPS], F32),
+            over.tile([P, PACK, GROUPS, P // GROUPS], F32, name="wgt_wide1", align_bytes=64, offset=24320),
+        ]
         wgt_sb = held("wgt_sb", [P, J], F32)
         wgo_sb = [held(f"wgo_sb{h}", [P, HALF], F32) for h in halves]
         wt_w = held("wt_w", [P, 2 * N], U8)
@@ -53,10 +62,10 @@ def tile_list_scatb_kernel(
         w_s = held("w_s", [P, 2 * N], U8)
         bias = held("bias", [P, N // P], F32)
         bias_rows = held("bias_rows", [P, P], F32)
-        win = [held(f"win{t}", [P, T], F32) for t in tiles]
-        ones = over.tile([P, PACK * P + PACK], BF16, name="ones", align_bytes=64, offset=1536)
+        win = {}
+        ones = over.tile([P, 2 * P + 2], F32, name="ones", align_bytes=64, offset=8192)
         eye = held("eye", [P, P], F32)
-        sel = over.tile([P, PACK, PACK * P], BF16, name="sel", align_bytes=64, offset=4096)
+        sel = held("sel", [P, PACK, PACK * P], BF16)
         sel_w = held("sel_w", [P, PACK * P], U32)
         sel_s = held("sel_s", [P, PACK * P], U8)
         names = ("x", "cq", "cr")
@@ -90,34 +99,43 @@ def tile_list_scatb_kernel(
                 in_=src[0, 4 * quad : 4 * quad + 4, :].bitcast(I32),
             )
 
-        nc.gpsimd.memset(ones[:].bitcast(I32), 0)
+        def zero_window(t, offset, pieces=1):
+            win[t] = over.tile([P, T], F32, name=f"win{t}", align_bytes=64, offset=offset)
+            for lo in range(0, T, T // pieces):
+                nc.gpsimd.memset(win[t][:, lo : lo + T // pieces].bitcast(I32), 0)
+
+        nc.gpsimd.memset(ones[:], 0.0)
+        nc.gpsimd.memset(wgt_rows[P // 2 : P, :], 0.0)
         nc.gpsimd.affine_select(
             out=ones[:],
             in_=ones[:],
-            pattern=[[1, PACK * P + PACK]],
+            pattern=[[1, 2 * P + 2]],
             compare_op=mybir.AluOpType.not_equal,
             fill=1.0,
-            base=-(PACK - 1),
-            channel_multiplier=-PACK,
+            base=-1,
+            channel_multiplier=-2,
         )
-        nc.gpsimd.memset(w_s[:].bitcast(I32), 0)
-        nc.gpsimd.memset(bias_rows[:], 0.0)
+        nc.vector.memset(w_s[:].bitcast(I32), 0)
+        nc.vector.memset(bias_rows[:], 0.0)
 
         nc.sync.dma_start(picks[:], offs)
+        nc.sync.dma_start(
+            out=wgt_rows[0 : P // 2, :], in_=wgt[0 : P : P // GROUPS, :].rearrange("g (b j) -> g b j", j=STRIP)
+        )
         load_c(0)
-        nc.sync.dma_start(out=wgt_sb[:], in_=wgt)
         load_x(0)
-        load_c(1)
-        for n in range(5):
-            load_scales(n)
-        load_x(1)
-        load_scales(5)
-        load_x(2)
-        load_scales(6)
-        load_scales(7)
         nc.sync.dma_start(out=bias_rows[0 : N // P, :], in_=b.rearrange("(t p) -> t p", p=P))
-        nc.sync.dma_start(places[:], offs2)
+        for n in range(2):
+            load_scales(n)
+        load_c(1)
+        load_x(1)
+        for n in range(2, 4):
+            load_scales(n)
+        load_x(2)
+        for n in range(4, 8):
+            load_scales(n)
         load_x(3)
+        nc.sync.dma_start(places[:], offs2)
         nc.sync.dma_start(out=wt_w[:].bitcast(I32), in_=wt_words[0].bitcast(I32))
         nc.sync.dma_start(out=wx_w[:].bitcast(I32), in_=wx_words[0].rearrange("p n t -> p (n t)").bitcast(I32))
         nc.sync.dma_start(out=wgo_sb[0][:], in_=wgo[:, 0:HALF])
@@ -125,12 +143,21 @@ def tile_list_scatb_kernel(
         load_c(3)
         nc.sync.dma_start(out=wgo_sb[1][:], in_=wgo[:, HALF:J])
 
+        placed = {("cq", 768): 67136, ("x", 256): 69120, ("x", 128): 70656, ("cq", 512): 71168, ("x", 512): 71168}
+
         def interleave(o, lo, hi, src, slot=None):
-            if o == "cq" and lo < HALF:
-                grouped[o, lo] = over.tile([P, hi - lo, PACK], BF16, name=f"g_cq{lo}", align_bytes=64, offset=2048 - 8 * lo)
+            if o == "cq" and lo == 0:
+                grouped[o, lo] = over.tile([P, hi - lo, PACK], BF16, name="g_cq0", align_bytes=64, offset=8128)
+            elif o == "cq" and lo == CHUNK:
+                grouped[o, lo] = inside_xg(2 * J - CHUNK, CHUNK)
+            elif o == "x" and lo == 0:
+                grouped[o, lo] = inside_xg(PACK * J - CHUNK, STRIP)
+            elif (o, lo) in placed:
+                grouped[o, lo] = over.tile([P, hi - lo, PACK], BF16, name=f"g_{o}{lo}", align_bytes=64, offset=placed[o, lo])
             else:
                 grouped[o, lo] = held(f"g_{o}{lo}", [P, hi - lo, PACK], BF16, slot=slot)
-            nc.scalar.copy(
+            copy = nc.vector.tensor_copy if (o, lo) == ("cq", 0) else nc.scalar.copy
+            copy(
                 out=grouped[o, lo][:].rearrange("p (a e) t -> p a t e", e=4),
                 in_=src.rearrange("p t (a e) -> p a t e", e=4),
             )
@@ -152,7 +179,7 @@ def tile_list_scatb_kernel(
 
         def decode(s):
             h, lo = divmod(s * STRIP, HALF)
-            dq[s] = ps_dq.tile([P, PACK, STRIP], F32, name="dq", tag="bank")
+            dq[s] = ps_dq.tile([P, PACK, STRIP], F32, name="dq", tag=f"bank{(0, 1, 3, 0, 0, 2, 2, 1)[s]}")
             for i in range(PACK):
                 nc.tensor.matmul_mx(
                     out=dq[s][:, i, :],
@@ -165,7 +192,12 @@ def tile_list_scatb_kernel(
                 )
 
         def residual_tile(q):
-            grouped["cr", q * CHUNK] = held(f"g_cr{q}", [P, CHUNK, PACK], BF16)
+            if q == 0:
+                grouped["cr", 0] = inside_xg((PACK - 1) * J, CHUNK)
+            elif q == 1:
+                grouped["cr", CHUNK] = over.tile([P, CHUNK, PACK], BF16, name="g_cr1", align_bytes=64, offset=73216)
+            else:
+                grouped["cr", q * CHUNK] = held(f"g_cr{q}", [P, CHUNK, PACK], BF16)
             return grouped["cr", q * CHUNK]
 
         def negate(s):
@@ -174,7 +206,7 @@ def tile_list_scatb_kernel(
 
         def subtract(s):
             q, lo = divmod(s * STRIP, CHUNK)
-            left[s] = ps_dq.tile([STRIP, PACK, P], F32, name="left", tag="bank")
+            left[s] = ps_dq.tile([STRIP, PACK, P], F32, name="left", tag=f"bank{(3, 0, 2, 1, 1, 3, 3, 2)[s]}")
             for i in range(PACK):
                 terms = (neg[s][:, i, :], c_raw[q][:, i, lo : lo + STRIP])
                 for n, term in enumerate(terms):
@@ -189,7 +221,7 @@ def tile_list_scatb_kernel(
         def turn_back(s):
             q, r = divmod(s, 2)
             if r == 0:
-                back[q] = ps_dq.tile([P, 2, 2, STRIP], F32, name="back", tag="bank")
+                back[q] = ps_dq.tile([P, 2, 2, STRIP], F32, name="back", tag=f"bank{(1, 3, 0, 1)[q]}")
             pairs = left_bf[s][:].rearrange("j u p e -> j (u p e)").bitcast(F32)
             for u in range(2):
                 nc.tensor.transpose(back[q][:, r, u, :], pairs[:, u * P : (u + 1) * P], eye[:])
@@ -215,25 +247,31 @@ def tile_list_scatb_kernel(
         def project(t, lo, hi):
             acc[t, lo] = ps_y.tile([P, hi - lo], F32, name="acc", tag="acc")
             ncols = slice(t * P, (t + 1) * P)
-            order = ("cr", "cq", "x") if lo >= HALF else ("cq", "cr", "x")
-            step = HALF if hi - lo == HALF else STRIP
-            for at in range(lo, hi, step):
+            order = ("cr", "cq", "x") if lo >= HALF else ("x", "cq", "cr")
+            passes = []
+            for o in order:
+                if o == "x":
+                    step = HALF if hi - lo == HALF else STRIP
+                    passes.extend((o, at, step) for at in range(lo, hi, step))
+                elif lo % CHUNK and hi - lo > STRIP:
+                    passes.extend([(o, lo, STRIP), (o, lo + STRIP, CHUNK)])
+                else:
+                    passes.append((o, lo, hi - lo))
+            for n, (o, at, step) in enumerate(passes):
                 h, first = divmod(at, HALF)
-                cols = slice(first, first + step)
-                for o in order:
-                    if o == "x":
-                        w, ws = wt_w[:, 2 * t * P : 2 * (t + 1) * P].bitcast(FP4X4), w_s[:, N + t * P : N + (t + 1) * P]
-                    else:
-                        w, ws = wx_w[:, ncols].bitcast(FP8X4), w_s[:, ncols]
-                    nc.tensor.matmul_mx(
-                        out=acc[t, lo][:, at - lo : at - lo + step],
-                        lhsT=w,
-                        lhsT_scale=ws,
-                        rhs=codes(o, at, at + step),
-                        rhs_scale=scales[o, h][:, cols],
-                        start=(o == order[0]),
-                        stop=(o == order[-1]),
-                    )
+                if o == "x":
+                    w, ws = wt_w[:, 2 * t * P : 2 * (t + 1) * P].bitcast(FP4X4), w_s[:, N + t * P : N + (t + 1) * P]
+                else:
+                    w, ws = wx_w[:, ncols].bitcast(FP8X4), w_s[:, ncols]
+                nc.tensor.matmul_mx(
+                    out=acc[t, lo][:, at - lo : at - lo + step],
+                    lhsT=w,
+                    lhsT_scale=ws,
+                    rhs=codes(o, at, at + step),
+                    rhs_scale=scales[o, h][:, first : first + step],
+                    start=(n == 0),
+                    stop=(n == len(passes) - 1),
+                )
 
         def finish(t, lo, hi, slot=None):
             ys[t, lo] = held(f"ys{t}_{lo}", [P, hi - lo], F32, slot=slot)
@@ -248,65 +286,91 @@ def tile_list_scatb_kernel(
             if hi == J:
                 nc.sync.dma_start(out=out[t * P : (t + 1) * P, :], in_=win[t][:])
 
-        for t in tiles:
-            nc.vector.memset(win[t][:], 0.0)
+        nc.vector.tensor_copy(out=eye[:], in_=ones[:, 1 : 2 * P : 2])
         for i in range(PACK):
-            nc.scalar.copy(out=sel[:, i, :], in_=ones[:, PACK - 1 - i : PACK - 1 - i + PACK * P])
-        nc.scalar.copy(out=eye[:], in_=ones[:, PACK - 1 : PACK * P : PACK])
+            nc.vector.tensor_copy(out=sel[:, i, :], in_=ones[:].bitcast(BF16)[:, PACK - 1 - i : PACK - 1 - i + PACK * P])
         nc.vector.quantize_mx(out=sel_w[:].bitcast(FP8X4), scales=sel_s[:], in_=sel[:].rearrange("p i m -> p (i m)"))
+        wgt_turned = ps_dq.tile([P, P], F32, name="wgt_turned", tag="bank0")
+        nc.tensor.transpose(wgt_turned[:], wgt_rows[:], eye[:])
+        wgt_back = {}
+        for h in halves:
+            picked = wgt_turned[:, 0 : P // 2].rearrange("j (g b) -> j b g", g=GROUPS)[:, h * PACK : (h + 1) * PACK, :]
+            nc.scalar.copy(
+                out=wgt_wide[h][:], in_=picked.unsqueeze(3).to_broadcast([P, PACK, GROUPS, P // GROUPS])
+            )
+            wgt_back[h] = ps_dq.tile([P, PACK, STRIP], F32, name="wgt_back", tag=f"bank{h + 1}")
+            for u in range(PACK):
+                nc.tensor.transpose(wgt_back[h][:, u, :], wgt_wide[h][:, u].rearrange("j g r -> j (g r)"), eye[:])
         interleave_c(0)
         quantize_chunk("cq", 0)
+        nc.vector.tensor_copy(out=wgt_sb[:, 0:HALF], in_=wgt_back[0][:].rearrange("p u j -> p (u j)"))
+        nc.scalar.copy(out=wgt_sb[:, HALF:J], in_=wgt_back[1][:].rearrange("p u j -> p (u j)"))
+        zero_window(1, 0, pieces=4)
+        zero_window(3, 26304, pieces=4)
 
-        xg = over.tile([P, 2 * PACK * HALF - STRIP], F32, name="xg", align_bytes=64, offset=2048)
-        xg_half = {
-            0: xg[:, PACK * HALF - STRIP : 2 * PACK * HALF - STRIP].rearrange("p (i j) -> p i j", i=PACK),
-            1: xg[:, 0 : PACK * HALF].rearrange("p (i j) -> p i j", i=PACK),
-        }
+        xg = over.tile([P, PACK * J], F32, name="xg", align_bytes=64, offset=8960)
+        xg_planes = xg[:].rearrange("p (i j) -> p i j", i=PACK)
+
+        def inside_xg(at, places):
+            return xg[:, at : at + 2 * places].bitcast(BF16).rearrange("p (j t) -> p j t", t=PACK)
 
         def gather(i, lo, hi):
-            h, at = divmod(lo, HALF)
             nc.vector.tensor_tensor(
-                xg_half[h][:, i, at : at + hi - lo],
+                xg[:, i * J + lo : i * J + hi],
                 x_pl[i][:].indirect(picks[:, lo // 16 : hi // 16]),
                 wgt_sb[:, lo:hi],
                 MULT,
             )
 
         def interleave_x(lo, hi, slot=None):
-            h, at = divmod(lo, HALF)
-            interleave("x", lo, hi, xg_half[h][:, :, at : at + hi - lo], slot=slot)
+            interleave("x", lo, hi, xg_planes[:, :, lo:hi], slot=slot)
+
+        def round_and_turn_strip(s):
+            round_left(s)
+            turn_back(s)
 
         gather(0, 0, HALF)
         gather(0, HALF, J)
+        zero_window(2, 34496, pieces=4)
         decode_and_negate(0)
-        interleave_c(1)
-        quantize_chunk("cq", 1)
-        round_and_turn(0)
-        decode_and_negate(1)
-        regroup(0)
-        round_and_turn(1)
-        regroup(1)
-        bias_turned = ps_dq.tile([P, P], F32, name="bias_turned", tag="bank")
+        bias_turned = ps_dq.tile([P, P], F32, name="bias_turned", tag="bank2")
         nc.tensor.transpose(bias_turned[:], bias_rows[:], eye[:])
         nc.scalar.copy(out=bias[:], in_=bias_turned[:, 0 : N // P])
-        for q in (0, 1):
-            gather(q + 1, 0, HALF)
-            gather(q + 1, HALF, J)
-            early_cr[q] = held(f"w_cr_early{q}", [P, CHUNK], U32, slot=f"x_pl{q + 1}")
-            quantize_chunk("cr", q)
+        interleave_c(1)
+        quantize_chunk("cq", 1)
+        round_left(0)
+        decode(2)
+        decode(3)
+        round_left(1)
+        turn_back(0)
+        turn_back(1)
+        negate(2)
+        negate(3)
+        regroup(0)
+        subtract(2)
+        subtract(3)
+        gather(1, 0, J)
+        zero_window(0, 58944, pieces=4)
+        gather(2, 0, J)
+        early_cr[0] = held("w_cr_early0", [P, CHUNK], U32, slot="x_pl2")
+        quantize_chunk("cr", 0)
         last = PACK - 1
         gather(last, 0, STRIP)
-        gather(last, STRIP, HALF)
+        gather(last, STRIP, HALF + STRIP)
+        round_and_turn(1)
         interleave_x(0, STRIP)
         quantize("x", 0, STRIP)
-        gather(last, HALF, J)
+        gather(last, HALF + STRIP, J)
         interleave_x(STRIP, CHUNK)
         quantize("x", STRIP, CHUNK)
         for t in tiles:
             project(t, 0, STRIP)
         finish(0, 0, STRIP)
+        regroup(1)
+        early_cr[1] = held("w_cr_early1", [P, CHUNK], U32)
+        quantize_chunk("cr", 1)
         finish(1, 0, STRIP)
-        interleave_x(CHUNK, HALF, slot=f"g_x{STRIP}")
+        interleave_x(CHUNK, HALF)
         quantize("x", CHUNK, HALF)
         finish(2, 0, STRIP)
         finish(3, 0, STRIP)
@@ -319,7 +383,7 @@ def tile_list_scatb_kernel(
         quantize_chunk("cq", 3)
         finish(1, STRIP, HALF)
         decode_and_negate(2)
-        interleave_x(2 * CHUNK, 3 * CHUNK, slot=f"g_cq{2 * CHUNK}")
+        interleave_x(2 * CHUNK, 3 * CHUNK)
         quantize_chunk("x", 2)
         round_and_turn(2)
         finish(2, STRIP, HALF)

@@ -45,10 +45,8 @@ def tile_list_scatb_kernel(
         chunks = range(J // CHUNK)
         tiles = range(N // P)
 
-        x_pl = [over.tile([P, T], F32, name="x_pl0", align_bytes=64, offset=42624)]
-        x_pl.append(over.tile([P, T], F32, name="x_pl1", align_bytes=64, offset=50816))
-        x_pl.append(held("x_pl2", [P, T], F32))
-        x_pl.append(over.tile([P, T], F32, name="x_pl3", align_bytes=64, offset=73216))
+        x_pl = [held(f"x_pl{i}", [P, T], F32) for i in range(PACK - 1)]
+        x_pl.append(over.tile([P, T], F32, name="x_pl3", align_bytes=64, offset=36864))
         c_raw = [held(f"c_raw{q}", [P, PACK, CHUNK], F32) for q in chunks]
         wgt_rows = held("wgt_rows", [P, STRIP], F32)
         wgt_wide = [
@@ -62,7 +60,7 @@ def tile_list_scatb_kernel(
         w_s = held("w_s", [P, 2 * N], U8)
         bias = held("bias", [P, N // P], F32)
         bias_rows = held("bias_rows", [P, P], F32)
-        win = {}
+        win = [held(f"win{t}", [P, T], F32) for t in tiles]
         ones = over.tile([P, 2 * P + 2], F32, name="ones", align_bytes=64, offset=8192)
         eye = held("eye", [P, P], F32)
         sel = held("sel", [P, PACK, PACK * P], BF16)
@@ -99,13 +97,7 @@ def tile_list_scatb_kernel(
                 in_=src[0, 4 * quad : 4 * quad + 4, :].bitcast(I32),
             )
 
-        def zero_window(t, offset, pieces=1):
-            win[t] = over.tile([P, T], F32, name=f"win{t}", align_bytes=64, offset=offset)
-            for lo in range(0, T, T // pieces):
-                nc.gpsimd.memset(win[t][:, lo : lo + T // pieces].bitcast(I32), 0)
-
         nc.gpsimd.memset(ones[:], 0.0)
-        nc.gpsimd.memset(wgt_rows[P // 2 : P, :], 0.0)
         nc.gpsimd.affine_select(
             out=ones[:],
             in_=ones[:],
@@ -117,6 +109,9 @@ def tile_list_scatb_kernel(
         )
         nc.vector.memset(w_s[:].bitcast(I32), 0)
         nc.vector.memset(bias_rows[:], 0.0)
+        nc.vector.memset(wgt_rows[P // 2 : P, :], 0.0)
+        for t in tiles:
+            nc.vector.memset(win[t][:].bitcast(I32), 0)
 
         nc.sync.dma_start(picks[:], offs)
         nc.sync.dma_start(
@@ -143,7 +138,7 @@ def tile_list_scatb_kernel(
         load_c(3)
         nc.sync.dma_start(out=wgo_sb[1][:], in_=wgo[:, HALF:J])
 
-        placed = {("cq", 768): 67136, ("x", 256): 69120, ("x", 128): 70656, ("cq", 512): 71168, ("x", 512): 71168}
+        placed = {("cq", 768): 28672, ("x", 256): 30656, ("x", 128): 32192, ("cq", 512): 32704, ("x", 512): 32704}
 
         def interleave(o, lo, hi, src, slot=None):
             if o == "cq" and lo == 0:
@@ -156,8 +151,7 @@ def tile_list_scatb_kernel(
                 grouped[o, lo] = over.tile([P, hi - lo, PACK], BF16, name=f"g_{o}{lo}", align_bytes=64, offset=placed[o, lo])
             else:
                 grouped[o, lo] = held(f"g_{o}{lo}", [P, hi - lo, PACK], BF16, slot=slot)
-            copy = nc.vector.tensor_copy if (o, lo) == ("cq", 0) else nc.scalar.copy
-            copy(
+            nc.scalar.copy(
                 out=grouped[o, lo][:].rearrange("p (a e) t -> p a t e", e=4),
                 in_=src.rearrange("p t (a e) -> p a t e", e=4),
             )
@@ -195,7 +189,7 @@ def tile_list_scatb_kernel(
             if q == 0:
                 grouped["cr", 0] = inside_xg((PACK - 1) * J, CHUNK)
             elif q == 1:
-                grouped["cr", CHUNK] = over.tile([P, CHUNK, PACK], BF16, name="g_cr1", align_bytes=64, offset=73216)
+                grouped["cr", CHUNK] = over.tile([P, CHUNK, PACK], BF16, name="g_cr1", align_bytes=64, offset=36864)
             else:
                 grouped["cr", q * CHUNK] = held(f"g_cr{q}", [P, CHUNK, PACK], BF16)
             return grouped["cr", q * CHUNK]
@@ -286,9 +280,9 @@ def tile_list_scatb_kernel(
             if hi == J:
                 nc.sync.dma_start(out=out[t * P : (t + 1) * P, :], in_=win[t][:])
 
-        nc.vector.tensor_copy(out=eye[:], in_=ones[:, 1 : 2 * P : 2])
+        nc.scalar.copy(out=eye[:], in_=ones[:, 1 : 2 * P : 2])
         for i in range(PACK):
-            nc.vector.tensor_copy(out=sel[:, i, :], in_=ones[:].bitcast(BF16)[:, PACK - 1 - i : PACK - 1 - i + PACK * P])
+            nc.scalar.copy(out=sel[:, i, :], in_=ones[:].bitcast(BF16)[:, PACK - 1 - i : PACK - 1 - i + PACK * P])
         nc.vector.quantize_mx(out=sel_w[:].bitcast(FP8X4), scales=sel_s[:], in_=sel[:].rearrange("p i m -> p (i m)"))
         wgt_turned = ps_dq.tile([P, P], F32, name="wgt_turned", tag="bank0")
         nc.tensor.transpose(wgt_turned[:], wgt_rows[:], eye[:])
@@ -303,10 +297,8 @@ def tile_list_scatb_kernel(
                 nc.tensor.transpose(wgt_back[h][:, u, :], wgt_wide[h][:, u].rearrange("j g r -> j (g r)"), eye[:])
         interleave_c(0)
         quantize_chunk("cq", 0)
-        nc.vector.tensor_copy(out=wgt_sb[:, 0:HALF], in_=wgt_back[0][:].rearrange("p u j -> p (u j)"))
+        nc.scalar.copy(out=wgt_sb[:, 0:HALF], in_=wgt_back[0][:].rearrange("p u j -> p (u j)"))
         nc.scalar.copy(out=wgt_sb[:, HALF:J], in_=wgt_back[1][:].rearrange("p u j -> p (u j)"))
-        zero_window(1, 0, pieces=4)
-        zero_window(3, 26304, pieces=4)
 
         xg = over.tile([P, PACK * J], F32, name="xg", align_bytes=64, offset=8960)
         xg_planes = xg[:].rearrange("p (i j) -> p i j", i=PACK)
@@ -331,7 +323,6 @@ def tile_list_scatb_kernel(
 
         gather(0, 0, HALF)
         gather(0, HALF, J)
-        zero_window(2, 34496, pieces=4)
         decode_and_negate(0)
         bias_turned = ps_dq.tile([P, P], F32, name="bias_turned", tag="bank2")
         nc.tensor.transpose(bias_turned[:], bias_rows[:], eye[:])
@@ -350,7 +341,6 @@ def tile_list_scatb_kernel(
         subtract(2)
         subtract(3)
         gather(1, 0, J)
-        zero_window(0, 58944, pieces=4)
         gather(2, 0, J)
         early_cr[0] = held("w_cr_early0", [P, CHUNK], U32, slot="x_pl2")
         quantize_chunk("cr", 0)

@@ -51,7 +51,7 @@ def tile_list_scatb_kernel(
         wgt_rows = held("wgt_rows", [P, STRIP], F32)
         wgt_wide = [
             held("wgt_wide0", [P, PACK, GROUPS, P // GROUPS], F32),
-            over.tile([P, PACK, GROUPS, P // GROUPS], F32, name="wgt_wide1", align_bytes=64, offset=24320),
+            over.tile([P, PACK, GROUPS, P // GROUPS], F32, name="wgt_wide1", align_bytes=64, offset=23808),
         ]
         wgt_sb = held("wgt_sb", [P, J], F32)
         wgo_sb = [held(f"wgo_sb{h}", [P, HALF], F32) for h in halves]
@@ -123,14 +123,14 @@ def tile_list_scatb_kernel(
         for n in range(2):
             load_scales(n)
         load_c(1)
-        load_x(1)
         for n in range(2, 4):
             load_scales(n)
-        load_x(2)
+        load_x(1)
         for n in range(4, 8):
             load_scales(n)
-        load_x(3)
+        load_x(2)
         nc.sync.dma_start(places[:], offs2)
+        load_x(3)
         nc.sync.dma_start(out=wt_w[:].bitcast(I32), in_=wt_words[0].bitcast(I32))
         nc.sync.dma_start(out=wx_w[:].bitcast(I32), in_=wx_words[0].rearrange("p n t -> p (n t)").bitcast(I32))
         nc.sync.dma_start(out=wgo_sb[0][:], in_=wgo[:, 0:HALF])
@@ -143,10 +143,9 @@ def tile_list_scatb_kernel(
         def interleave(o, lo, hi, src, slot=None):
             if o == "cq" and lo == 0:
                 grouped[o, lo] = over.tile([P, hi - lo, PACK], BF16, name="g_cq0", align_bytes=64, offset=8128)
-            elif o == "cq" and lo == CHUNK:
-                grouped[o, lo] = inside_xg(2 * J - CHUNK, CHUNK)
-            elif o == "x" and lo == 0:
-                grouped[o, lo] = inside_xg(PACK * J - CHUNK, STRIP)
+            elif o == "cq" and lo < HALF:
+                at = xg_base[(lo - CHUNK) // STRIP] + 2 * HALF - STRIP
+                grouped[o, lo] = xg[:, at : at + CHUNK].bitcast(BF16).rearrange("p (j t) -> p j t", t=PACK)
             elif (o, lo) in placed:
                 grouped[o, lo] = over.tile([P, hi - lo, PACK], BF16, name=f"g_{o}{lo}", align_bytes=64, offset=placed[o, lo])
             else:
@@ -186,9 +185,7 @@ def tile_list_scatb_kernel(
                 )
 
         def residual_tile(q):
-            if q == 0:
-                grouped["cr", 0] = inside_xg((PACK - 1) * J, CHUNK)
-            elif q == 1:
+            if q == 1:
                 grouped["cr", CHUNK] = over.tile([P, CHUNK, PACK], BF16, name="g_cr1", align_bytes=64, offset=36864)
             else:
                 grouped["cr", q * CHUNK] = held(f"g_cr{q}", [P, CHUNK, PACK], BF16)
@@ -300,22 +297,22 @@ def tile_list_scatb_kernel(
         nc.scalar.copy(out=wgt_sb[:, 0:HALF], in_=wgt_back[0][:].rearrange("p u j -> p (u j)"))
         nc.scalar.copy(out=wgt_sb[:, HALF:J], in_=wgt_back[1][:].rearrange("p u j -> p (u j)"))
 
-        xg = over.tile([P, PACK * J], F32, name="xg", align_bytes=64, offset=8960)
-        xg_planes = xg[:].rearrange("p (i j) -> p i j", i=PACK)
-
-        def inside_xg(at, places):
-            return xg[:, at : at + 2 * places].bitcast(BF16).rearrange("p (j t) -> p j t", t=PACK)
+        xg = over.tile([P, PACK * J - STRIP], F32, name="xg", align_bytes=64, offset=8960)
+        xg_base = (PACK * HALF - STRIP, 0)
+        xg_half = [xg[:, at : at + PACK * HALF].rearrange("p (i j) -> p i j", i=PACK) for at in xg_base]
 
         def gather(i, lo, hi):
+            h, at = divmod(lo, HALF)
             nc.vector.tensor_tensor(
-                xg[:, i * J + lo : i * J + hi],
+                xg_half[h][:, i, at : at + hi - lo],
                 x_pl[i][:].indirect(picks[:, lo // 16 : hi // 16]),
                 wgt_sb[:, lo:hi],
                 MULT,
             )
 
         def interleave_x(lo, hi, slot=None):
-            interleave("x", lo, hi, xg_planes[:, :, lo:hi], slot=slot)
+            h, at = divmod(lo, HALF)
+            interleave("x", lo, hi, xg_half[h][:, :, at : at + hi - lo], slot=slot)
 
         def round_and_turn_strip(s):
             round_left(s)
@@ -327,8 +324,9 @@ def tile_list_scatb_kernel(
         bias_turned = ps_dq.tile([P, P], F32, name="bias_turned", tag="bank2")
         nc.tensor.transpose(bias_turned[:], bias_rows[:], eye[:])
         nc.scalar.copy(out=bias[:], in_=bias_turned[:, 0 : N // P])
-        interleave_c(1)
-        quantize_chunk("cq", 1)
+        for lo in (CHUNK, CHUNK + STRIP):
+            interleave("cq", lo, lo + STRIP, c_raw[1][:, :, lo - CHUNK : lo - CHUNK + STRIP])
+            quantize("cq", lo, lo + STRIP)
         round_left(0)
         decode(2)
         decode(3)
@@ -340,17 +338,18 @@ def tile_list_scatb_kernel(
         regroup(0)
         subtract(2)
         subtract(3)
-        gather(1, 0, J)
-        gather(2, 0, J)
+        for i in (1, 2):
+            gather(i, 0, HALF)
+            gather(i, HALF, J)
         early_cr[0] = held("w_cr_early0", [P, CHUNK], U32, slot="x_pl2")
         quantize_chunk("cr", 0)
         last = PACK - 1
         gather(last, 0, STRIP)
-        gather(last, STRIP, HALF + STRIP)
+        gather(last, STRIP, HALF)
         round_and_turn(1)
         interleave_x(0, STRIP)
         quantize("x", 0, STRIP)
-        gather(last, HALF + STRIP, J)
+        gather(last, HALF, J)
         interleave_x(STRIP, CHUNK)
         quantize("x", STRIP, CHUNK)
         for t in tiles:
@@ -390,9 +389,10 @@ def tile_list_scatb_kernel(
         regroup(3)
         quantize_chunk("cr", 3)
         finish(1, HALF, 3 * CHUNK, slot="left_bf7")
-        for t in (0, 1):
+        project(2, HALF, 3 * CHUNK)
+        finish(2, HALF, 3 * CHUNK)
+        for t in (0, 1, 2):
             project(t, 3 * CHUNK, J)
             finish(t, 3 * CHUNK, J)
-        for t in (2, 3):
-            project(t, HALF, J)
-            finish(t, HALF, J)
+        project(3, HALF, J)
+        finish(3, HALF, J)

@@ -3,7 +3,7 @@ from contextlib import ExitStack
 import concourse.mybir as mybir
 
 K, L, N, T, J = 512, 512, 512, 2048, 1024
-FLOPS = 4 * 2 * 512 * 512 * 1024
+FLOPS = 2 * J * (K * N + 2 * L * N + L * L)
 
 F32 = mybir.dt.float32
 BF16 = mybir.dt.bfloat16
@@ -20,15 +20,44 @@ IDENT = mybir.ActivationFunctionType.Identity
 P = 128
 PACK = 4
 HALF = 512
-CHUNK = 256
+QUARTER = 256
 STRIP = 128
 GROUPS = 8
+
+QUARTER_BYTES = QUARTER * PACK * 2
+XG_COLUMNS = PACK * J - STRIP
+CQ0_AT = 0
+ONES_AT = CQ0_AT + 64
+XG_AT = CQ0_AT + 832
+WIDE1_AT = XG_AT + 4 * XG_COLUMNS - 1024
+CQ3_AT = CQ0_AT + 20544
+X1_AT = CQ3_AT + QUARTER_BYTES - 64
+X_STRIP1_AT = X1_AT + QUARTER_BYTES - 512
+CQ2_AT = X1_AT + QUARTER_BYTES
+CR1_AT = CQ0_AT + 28736
+
+BANK_TENANTS = (
+    ("wgt_turned", "dq0", "left1", "dq3", "dq4", "back2"),
+    ("wgt_back0", "dq1", "back0", "left3", "left4", "dq7", "back3"),
+    ("wgt_back1", "bias_turned", "left2", "dq5", "dq6", "left7"),
+    ("left0", "dq2", "back1", "left5", "left6"),
+)
 
 
 def tile_list_scatb_kernel(
     tc, xT, wgt, wt_words, wt_scales, c, wx_words, wx_scales, b, wgo, offs, offs2, out
 ):
     nc = tc.nc
+    bank = {tenant: f"bank{n}" for n, tenants in enumerate(BANK_TENANTS) for tenant in tenants}
+    placed = {
+        ("x", 0): CR1_AT,
+        ("cq", 0): CQ0_AT,
+        ("cq", 3 * QUARTER): CQ3_AT,
+        ("x", QUARTER): X1_AT,
+        ("x", STRIP): X_STRIP1_AT,
+        ("cq", 2 * QUARTER): CQ2_AT,
+        ("x", 2 * QUARTER): CQ2_AT,
+    }
     with ExitStack() as ctx:
         lists = ctx.enter_context(tc.tile_pool(name="lists", bufs=1))
         keep = ctx.enter_context(tc.tile_pool(name="keep", bufs=1))
@@ -42,16 +71,15 @@ def tile_list_scatb_kernel(
         picks = lists.tile([P, J // 16], U16, name="picks")
         places = lists.tile([P, J // 16], U16, name="places")
         halves = range(J // HALF)
-        chunks = range(J // CHUNK)
+        quarters = range(J // QUARTER)
         tiles = range(N // P)
 
-        x_pl = [held(f"x_pl{i}", [P, T], F32) for i in range(PACK - 1)]
-        x_pl.append(over.tile([P, T], F32, name="x_pl3", align_bytes=64, offset=36864))
-        c_raw = [held(f"c_raw{q}", [P, PACK, CHUNK], F32) for q in chunks]
+        x_pl = [held(f"x_pl{i}", [P, T], F32) for i in range(PACK)]
+        c_raw = [held(f"c_raw{q}", [P, PACK, QUARTER], F32) for q in quarters]
         wgt_rows = held("wgt_rows", [P, STRIP], F32)
         wgt_wide = [
             held("wgt_wide0", [P, PACK, GROUPS, P // GROUPS], F32),
-            over.tile([P, PACK, GROUPS, P // GROUPS], F32, name="wgt_wide1", align_bytes=64, offset=23808),
+            over.tile([P, PACK, GROUPS, P // GROUPS], F32, name="wgt_wide1", align_bytes=64, offset=WIDE1_AT),
         ]
         wgt_sb = held("wgt_sb", [P, J], F32)
         wgo_sb = [held(f"wgo_sb{h}", [P, HALF], F32) for h in halves]
@@ -61,41 +89,40 @@ def tile_list_scatb_kernel(
         bias = held("bias", [P, N // P], F32)
         bias_rows = held("bias_rows", [P, P], F32)
         win = [held(f"win{t}", [P, T], F32) for t in tiles]
-        ones = over.tile([P, 2 * P + 2], F32, name="ones", align_bytes=64, offset=8192)
+        ones = over.tile([P, 2 * P + 2], F32, name="ones", align_bytes=64, offset=ONES_AT)
         eye = held("eye", [P, P], F32)
         sel = held("sel", [P, PACK, PACK * P], BF16)
         sel_w = held("sel_w", [P, PACK * P], U32)
         sel_s = held("sel_s", [P, PACK * P], U8)
-        names = ("x", "cq", "cr")
-        words = {(o, h): held(f"w_{o}{h}", [P, HALF], U32) for o in names for h in halves if (o, h) != ("cr", 0)}
+        operands = ("x", "cq", "cr")
+        words = {(o, h): held(f"w_{o}{h}", [P, HALF], U32) for o in operands for h in halves if (o, h) != ("cr", 0)}
         early_cr = {}
 
         def codes(o, lo, hi):
             if o == "cr" and lo < HALF:
-                q, at = divmod(lo, CHUNK)
+                q, at = divmod(lo, QUARTER)
                 return early_cr[q][:, at : at + hi - lo].bitcast(FP8X4)
             h, at = divmod(lo, HALF)
             return words[o, h][:, at : at + hi - lo].bitcast(FP8X4)
 
-        scales = {(o, h): held(f"s_{o}{h}", [P, HALF], U8) for o in names for h in halves}
+        scales = {(o, h): held(f"s_{o}{h}", [P, HALF], U8) for o in operands for h in halves}
         grouped, ys, acc, dq, neg, left, left_bf, back = {}, {}, {}, {}, {}, {}, {}, {}
 
         x_src = xT.rearrange("(p i) t -> i p t", i=PACK)
         c_src = c.rearrange("(p i) j -> p i j", i=PACK)
 
         def load_c(q):
-            nc.sync.dma_start(out=c_raw[q][:], in_=c_src[:, :, q * CHUNK : (q + 1) * CHUNK])
+            nc.sync.dma_start(out=c_raw[q][:], in_=c_src[:, :, q * QUARTER : (q + 1) * QUARTER])
 
         def load_x(i):
             nc.sync.dma_start(out=x_pl[i][:], in_=x_src[i])
 
-        def load_scales(n):
-            which, quad = divmod(n, 4)
-            src = (wx_scales, wt_scales)[which]
-            nc.sync.dma_start(
-                out=w_s[32 * quad : 32 * quad + 4, which * N : (which + 1) * N].bitcast(I32),
-                in_=src[0, 4 * quad : 4 * quad + 4, :].bitcast(I32),
-            )
+        def load_scales(src, column, quads):
+            for quad in quads:
+                nc.sync.dma_start(
+                    out=w_s[32 * quad : 32 * quad + 4, column : column + N].bitcast(I32),
+                    in_=src[0, 4 * quad : 4 * quad + 4, :].bitcast(I32),
+                )
 
         nc.gpsimd.memset(ones[:], 0.0)
         nc.gpsimd.affine_select(
@@ -120,14 +147,11 @@ def tile_list_scatb_kernel(
         load_c(0)
         load_x(0)
         nc.sync.dma_start(out=bias_rows[0 : N // P, :], in_=b.rearrange("(t p) -> t p", p=P))
-        for n in range(2):
-            load_scales(n)
+        load_scales(wx_scales, 0, (0, 1))
         load_c(1)
-        for n in range(2, 4):
-            load_scales(n)
+        load_scales(wx_scales, 0, (2, 3))
         load_x(1)
-        for n in range(4, 8):
-            load_scales(n)
+        load_scales(wt_scales, N, range(4))
         load_x(2)
         nc.sync.dma_start(places[:], offs2)
         load_x(3)
@@ -138,16 +162,14 @@ def tile_list_scatb_kernel(
         load_c(3)
         nc.sync.dma_start(out=wgo_sb[1][:], in_=wgo[:, HALF:J])
 
-        placed = {("cq", 768): 28672, ("x", 256): 30656, ("x", 128): 32192, ("cq", 512): 32704, ("x", 512): 32704}
-
         def interleave(o, lo, hi, src, slot=None):
-            if o == "cq" and lo == 0:
-                grouped[o, lo] = over.tile([P, hi - lo, PACK], BF16, name="g_cq0", align_bytes=64, offset=8128)
-            elif o == "cq" and lo < HALF:
-                at = xg_base[(lo - CHUNK) // STRIP] + 2 * HALF - STRIP
-                grouped[o, lo] = xg[:, at : at + CHUNK].bitcast(BF16).rearrange("p (j t) -> p j t", t=PACK)
-            elif (o, lo) in placed:
-                grouped[o, lo] = over.tile([P, hi - lo, PACK], BF16, name=f"g_{o}{lo}", align_bytes=64, offset=placed[o, lo])
+            if (o, lo) in placed:
+                grouped[o, lo] = over.tile(
+                    [P, hi - lo, PACK], BF16, name=f"g_{o}{lo}", align_bytes=64, offset=placed[o, lo]
+                )
+            elif o == "cq":
+                at = xg_base[(lo - QUARTER) // STRIP] + 2 * HALF - STRIP
+                grouped[o, lo] = xg[:, at : at + 2 * STRIP].bitcast(BF16).rearrange("p (j t) -> p j t", t=PACK)
             else:
                 grouped[o, lo] = held(f"g_{o}{lo}", [P, hi - lo, PACK], BF16, slot=slot)
             nc.scalar.copy(
@@ -157,22 +179,21 @@ def tile_list_scatb_kernel(
 
         def quantize(o, lo, hi):
             h, at = divmod(lo, HALF)
-            cols = slice(at, at + hi - lo)
             nc.vector.quantize_mx(
                 out=codes(o, lo, hi),
-                scales=scales[o, h][:, cols],
+                scales=scales[o, h][:, at : at + hi - lo],
                 in_=grouped[o, lo][:].rearrange("p j t -> p (j t)"),
             )
 
         def interleave_c(q):
-            interleave("cq", q * CHUNK, (q + 1) * CHUNK, c_raw[q][:])
+            interleave("cq", q * QUARTER, (q + 1) * QUARTER, c_raw[q][:])
 
-        def quantize_chunk(o, q):
-            quantize(o, q * CHUNK, (q + 1) * CHUNK)
+        def quantize_quarter(o, q):
+            quantize(o, q * QUARTER, (q + 1) * QUARTER)
 
         def decode(s):
             h, lo = divmod(s * STRIP, HALF)
-            dq[s] = ps_dq.tile([P, PACK, STRIP], F32, name="dq", tag=f"bank{(0, 1, 3, 0, 0, 2, 2, 1)[s]}")
+            dq[s] = ps_dq.tile([P, PACK, STRIP], F32, name="dq", tag=bank[f"dq{s}"])
             for i in range(PACK):
                 nc.tensor.matmul_mx(
                     out=dq[s][:, i, :],
@@ -184,20 +205,13 @@ def tile_list_scatb_kernel(
                     stop=True,
                 )
 
-        def residual_tile(q):
-            if q == 1:
-                grouped["cr", CHUNK] = over.tile([P, CHUNK, PACK], BF16, name="g_cr1", align_bytes=64, offset=36864)
-            else:
-                grouped["cr", q * CHUNK] = held(f"g_cr{q}", [P, CHUNK, PACK], BF16)
-            return grouped["cr", q * CHUNK]
-
         def negate(s):
             neg[s] = held(f"neg{s}", [P, PACK, STRIP], F32, slot=f"neg{s % 2}")
             nc.scalar.activation(out=neg[s][:], in_=dq[s][:], func=COPY, scale=-1.0)
 
         def subtract(s):
-            q, lo = divmod(s * STRIP, CHUNK)
-            left[s] = ps_dq.tile([STRIP, PACK, P], F32, name="left", tag=f"bank{(3, 0, 2, 1, 1, 3, 3, 2)[s]}")
+            q, lo = divmod(s * STRIP, QUARTER)
+            left[s] = ps_dq.tile([STRIP, PACK, P], F32, name="left", tag=bank[f"left{s}"])
             for i in range(PACK):
                 terms = (neg[s][:, i, :], c_raw[q][:, i, lo : lo + STRIP])
                 for n, term in enumerate(terms):
@@ -212,18 +226,23 @@ def tile_list_scatb_kernel(
         def turn_back(s):
             q, r = divmod(s, 2)
             if r == 0:
-                back[q] = ps_dq.tile([P, 2, 2, STRIP], F32, name="back", tag=f"bank{(1, 3, 0, 1)[q]}")
+                back[q] = ps_dq.tile([P, 2, 2, STRIP], F32, name="back", tag=bank[f"back{q}"])
             pairs = left_bf[s][:].rearrange("j u p e -> j (u p e)").bitcast(F32)
             for u in range(2):
                 nc.tensor.transpose(back[q][:, r, u, :], pairs[:, u * P : (u + 1) * P], eye[:])
 
         def regroup(q):
+            if q == 1:
+                dst = over.tile([P, QUARTER, PACK], BF16, name="g_cr1", align_bytes=64, offset=CR1_AT)
+            else:
+                dst = held(f"g_cr{q}", [P, QUARTER, PACK], BF16)
+            grouped["cr", q * QUARTER] = dst
             nc.scalar.copy(
-                out=residual_tile(q)[:].bitcast(F32).rearrange("p (r j) u -> p r j u", r=2),
+                out=dst[:].bitcast(F32).rearrange("p (r j) u -> p r j u", r=2),
                 in_=back[q][:].rearrange("p r u j -> p r j u"),
             )
 
-        def decode_and_negate(q):
+        def decode_and_subtract(q):
             for s in (2 * q, 2 * q + 1):
                 decode(s)
             for s in (2 * q, 2 * q + 1):
@@ -244,8 +263,8 @@ def tile_list_scatb_kernel(
                 if o == "x":
                     step = HALF if hi - lo == HALF else STRIP
                     passes.extend((o, at, step) for at in range(lo, hi, step))
-                elif lo % CHUNK and hi - lo > STRIP:
-                    passes.extend([(o, lo, STRIP), (o, lo + STRIP, CHUNK)])
+                elif lo % QUARTER and hi - lo > STRIP:
+                    passes.extend([(o, lo, STRIP), (o, lo + STRIP, QUARTER)])
                 else:
                     passes.append((o, lo, hi - lo))
             for n, (o, at, step) in enumerate(passes):
@@ -281,23 +300,22 @@ def tile_list_scatb_kernel(
         for i in range(PACK):
             nc.scalar.copy(out=sel[:, i, :], in_=ones[:].bitcast(BF16)[:, PACK - 1 - i : PACK - 1 - i + PACK * P])
         nc.vector.quantize_mx(out=sel_w[:].bitcast(FP8X4), scales=sel_s[:], in_=sel[:].rearrange("p i m -> p (i m)"))
-        wgt_turned = ps_dq.tile([P, P], F32, name="wgt_turned", tag="bank0")
+
+        wgt_turned = ps_dq.tile([P, P], F32, name="wgt_turned", tag=bank["wgt_turned"])
         nc.tensor.transpose(wgt_turned[:], wgt_rows[:], eye[:])
         wgt_back = {}
         for h in halves:
-            picked = wgt_turned[:, 0 : P // 2].rearrange("j (g b) -> j b g", g=GROUPS)[:, h * PACK : (h + 1) * PACK, :]
-            nc.scalar.copy(
-                out=wgt_wide[h][:], in_=picked.unsqueeze(3).to_broadcast([P, PACK, GROUPS, P // GROUPS])
-            )
-            wgt_back[h] = ps_dq.tile([P, PACK, STRIP], F32, name="wgt_back", tag=f"bank{h + 1}")
+            strips = wgt_turned[:, 0 : P // 2].rearrange("j (g b) -> j b g", g=GROUPS)[:, h * PACK : (h + 1) * PACK, :]
+            nc.scalar.copy(out=wgt_wide[h][:], in_=strips.unsqueeze(3).to_broadcast([P, PACK, GROUPS, P // GROUPS]))
+            wgt_back[h] = ps_dq.tile([P, PACK, STRIP], F32, name="wgt_back", tag=bank[f"wgt_back{h}"])
             for u in range(PACK):
                 nc.tensor.transpose(wgt_back[h][:, u, :], wgt_wide[h][:, u].rearrange("j g r -> j (g r)"), eye[:])
         interleave_c(0)
-        quantize_chunk("cq", 0)
-        nc.scalar.copy(out=wgt_sb[:, 0:HALF], in_=wgt_back[0][:].rearrange("p u j -> p (u j)"))
-        nc.scalar.copy(out=wgt_sb[:, HALF:J], in_=wgt_back[1][:].rearrange("p u j -> p (u j)"))
+        quantize_quarter("cq", 0)
+        for h in halves:
+            nc.scalar.copy(out=wgt_sb[:, h * HALF : (h + 1) * HALF], in_=wgt_back[h][:].rearrange("p u j -> p (u j)"))
 
-        xg = over.tile([P, PACK * J - STRIP], F32, name="xg", align_bytes=64, offset=8960)
+        xg = over.tile([P, XG_COLUMNS], F32, name="xg", align_bytes=64, offset=XG_AT)
         xg_base = (PACK * HALF - STRIP, 0)
         xg_half = [xg[:, at : at + PACK * HALF].rearrange("p (i j) -> p i j", i=PACK) for at in xg_base]
 
@@ -314,18 +332,14 @@ def tile_list_scatb_kernel(
             h, at = divmod(lo, HALF)
             interleave("x", lo, hi, xg_half[h][:, :, at : at + hi - lo], slot=slot)
 
-        def round_and_turn_strip(s):
-            round_left(s)
-            turn_back(s)
-
         gather(0, 0, HALF)
         gather(0, HALF, J)
-        decode_and_negate(0)
-        bias_turned = ps_dq.tile([P, P], F32, name="bias_turned", tag="bank2")
+        decode_and_subtract(0)
+        bias_turned = ps_dq.tile([P, P], F32, name="bias_turned", tag=bank["bias_turned"])
         nc.tensor.transpose(bias_turned[:], bias_rows[:], eye[:])
         nc.scalar.copy(out=bias[:], in_=bias_turned[:, 0 : N // P])
-        for lo in (CHUNK, CHUNK + STRIP):
-            interleave("cq", lo, lo + STRIP, c_raw[1][:, :, lo - CHUNK : lo - CHUNK + STRIP])
+        for lo in (QUARTER, QUARTER + STRIP):
+            interleave("cq", lo, lo + STRIP, c_raw[1][:, :, lo - QUARTER : lo - QUARTER + STRIP])
             quantize("cq", lo, lo + STRIP)
         round_left(0)
         decode(2)
@@ -341,8 +355,9 @@ def tile_list_scatb_kernel(
         for i in (1, 2):
             gather(i, 0, HALF)
             gather(i, HALF, J)
-        early_cr[0] = held("w_cr_early0", [P, CHUNK], U32, slot="x_pl2")
-        quantize_chunk("cr", 0)
+        early_cr[0] = held("w_cr_early0", [P, QUARTER], U32, slot="x_pl2")
+        quantize_quarter("cr", 0)
+
         last = PACK - 1
         gather(last, 0, STRIP)
         gather(last, STRIP, HALF)
@@ -350,49 +365,51 @@ def tile_list_scatb_kernel(
         interleave_x(0, STRIP)
         quantize("x", 0, STRIP)
         gather(last, HALF, J)
-        interleave_x(STRIP, CHUNK)
-        quantize("x", STRIP, CHUNK)
+        interleave_x(STRIP, QUARTER)
+        quantize("x", STRIP, QUARTER)
         for t in tiles:
             project(t, 0, STRIP)
-        finish(0, 0, STRIP)
         regroup(1)
-        early_cr[1] = held("w_cr_early1", [P, CHUNK], U32)
-        quantize_chunk("cr", 1)
+        early_cr[1] = held("w_cr_early1", [P, QUARTER], U32)
+        quantize_quarter("cr", 1)
+        finish(0, 0, STRIP)
         finish(1, 0, STRIP)
-        interleave_x(CHUNK, HALF)
-        quantize("x", CHUNK, HALF)
+        interleave_x(QUARTER, HALF)
+        quantize_quarter("x", 1)
         finish(2, 0, STRIP)
         finish(3, 0, STRIP)
+
         for t in tiles:
             project(t, STRIP, HALF)
         interleave_c(2)
-        quantize_chunk("cq", 2)
+        quantize_quarter("cq", 2)
         finish(0, STRIP, HALF)
         interleave_c(3)
-        quantize_chunk("cq", 3)
+        quantize_quarter("cq", 3)
         finish(1, STRIP, HALF)
-        decode_and_negate(2)
-        interleave_x(2 * CHUNK, 3 * CHUNK)
-        quantize_chunk("x", 2)
+        decode_and_subtract(2)
+        interleave_x(2 * QUARTER, 3 * QUARTER)
+        quantize_quarter("x", 2)
         round_and_turn(2)
         finish(2, STRIP, HALF)
-        decode_and_negate(3)
+        decode_and_subtract(3)
         regroup(2)
-        quantize_chunk("cr", 2)
+        quantize_quarter("cr", 2)
         finish(3, STRIP, HALF, slot="left_bf5")
+
         for t in (0, 1):
-            project(t, HALF, 3 * CHUNK)
-        interleave_x(3 * CHUNK, J, slot="left_bf4")
-        quantize_chunk("x", 3)
-        finish(0, HALF, 3 * CHUNK)
+            project(t, HALF, 3 * QUARTER)
+        interleave_x(3 * QUARTER, J, slot="left_bf4")
+        quantize_quarter("x", 3)
+        finish(0, HALF, 3 * QUARTER)
         round_and_turn(3)
         regroup(3)
-        quantize_chunk("cr", 3)
-        finish(1, HALF, 3 * CHUNK, slot="left_bf7")
-        project(2, HALF, 3 * CHUNK)
-        finish(2, HALF, 3 * CHUNK)
+        quantize_quarter("cr", 3)
+        finish(1, HALF, 3 * QUARTER, slot="left_bf7")
+        project(2, HALF, 3 * QUARTER)
+        finish(2, HALF, 3 * QUARTER)
         for t in (0, 1, 2):
-            project(t, 3 * CHUNK, J)
-            finish(t, 3 * CHUNK, J)
+            project(t, 3 * QUARTER, J)
+            finish(t, 3 * QUARTER, J)
         project(3, HALF, J)
         finish(3, HALF, J)

@@ -257,13 +257,10 @@ def tile_list_scatb_kernel(
         def project(t, lo, hi):
             acc[t, lo] = ps_y.tile([P, hi - lo], F32, name="acc", tag="acc")
             ncols = slice(t * P, (t + 1) * P)
-            order = ("cr", "cq", "x") if lo >= HALF else ("x", "cq", "cr")
+            order = ("cr", "cq", "x") if lo == HALF else ("x", "cq", "cr") if lo < HALF else ("cq", "x", "cr")
             passes = []
             for o in order:
-                if o == "x":
-                    step = HALF if hi - lo == HALF else STRIP
-                    passes.extend((o, at, step) for at in range(lo, hi, step))
-                elif lo % QUARTER and hi - lo > STRIP:
+                if lo % QUARTER and hi - lo > STRIP:
                     passes.extend([(o, lo, STRIP), (o, lo + STRIP, QUARTER)])
                 else:
                     passes.append((o, lo, hi - lo))
@@ -406,10 +403,9 @@ def tile_list_scatb_kernel(
         regroup(3)
         quantize_quarter("cr", 3)
         finish(1, HALF, 3 * QUARTER, slot="left_bf7")
-        project(2, HALF, 3 * QUARTER)
-        finish(2, HALF, 3 * QUARTER)
-        for t in (0, 1, 2):
+        for t in (0, 1):
             project(t, 3 * QUARTER, J)
             finish(t, 3 * QUARTER, J)
-        project(3, HALF, J)
-        finish(3, HALF, J)
+        for t in (2, 3):
+            project(t, HALF, J)
+            finish(t, HALF, J)

@@ -294,8 +294,12 @@ def tile_list_scatb_kernel(
                 nc.sync.dma_start(out=out[t * P : (t + 1) * P, :], in_=win[t][:])
 
         nc.scalar.copy(out=eye[:], in_=ones[:, 1 : 2 * P : 2])
-        for i in range(PACK):
-            nc.scalar.copy(out=sel[:, i, :], in_=ones[:].bitcast(BF16)[:, PACK - 1 - i : PACK - 1 - i + PACK * P])
+        sel_words = sel[:].rearrange("p i m -> p (i m)").bitcast(U32)
+        plane = 2 * P
+        nc.scalar.copy(out=sel[:, 2, :], in_=ones[:].bitcast(BF16)[:, 1 : 1 + PACK * P])
+        nc.scalar.copy(out=sel_words[:, 3 * plane : 4 * plane], in_=ones[:].bitcast(U32)[:, 0:plane])
+        nc.scalar.copy(out=sel_words[:, plane : 2 * plane], in_=ones[:].bitcast(U32)[:, 1 : plane + 1])
+        nc.scalar.copy(out=sel_words[:, 0:plane], in_=sel_words[:, 2 * plane + 1 : 3 * plane + 1])
         nc.vector.quantize_mx(out=sel_w[:].bitcast(FP8X4), scales=sel_s[:], in_=sel[:].rearrange("p i m -> p (i m)"))
 
         wgt_turned = ps_dq.tile([P, P], F32, name="wgt_turned", tag=bank["wgt_turned"])

@@ -153,10 +153,10 @@ def tile_list_scatb_kernel(
         load_x(1)
         load_scales(wt_scales, N, range(4))
         load_x(2)
-        nc.sync.dma_start(places[:], offs2)
         load_x(3)
         nc.sync.dma_start(out=wt_w[:].bitcast(I32), in_=wt_words[0].bitcast(I32))
         nc.sync.dma_start(out=wx_w[:].bitcast(I32), in_=wx_words[0].rearrange("p n t -> p (n t)").bitcast(I32))
+        nc.sync.dma_start(places[:], offs2)
         nc.sync.dma_start(out=wgo_sb[0][:], in_=wgo[:, 0:HALF])
         load_c(2)
         load_c(3)
@@ -353,11 +353,12 @@ def tile_list_scatb_kernel(
         regroup(0)
         subtract(2)
         subtract(3)
-        for i in (1, 2):
-            gather(i, 0, HALF)
-            gather(i, HALF, J)
-        early_cr[0] = held("w_cr_early0", [P, QUARTER], U32, slot="x_pl2")
+        gather(1, 0, HALF)
+        gather(1, HALF, J)
+        gather(2, 0, HALF)
+        early_cr[0] = held("w_cr_early0", [P, QUARTER], U32, slot="x_pl1")
         quantize_quarter("cr", 0)
+        gather(2, HALF, J)
 
         last = PACK - 1
         gather(last, 0, STRIP)

@@ -26,7 +26,8 @@ GROUPS = 8
 
 QUARTER_BYTES = QUARTER * PACK * 2
 XG_COLUMNS = PACK * J - STRIP
-CQ0_AT = 0
+WIN3_AT = 0
+CQ0_AT = WIN3_AT + 4 * T - 64
 ONES_AT = CQ0_AT + 64
 XG_AT = CQ0_AT + 832
 WIDE1_AT = XG_AT + 4 * XG_COLUMNS - 1024
@@ -88,7 +89,8 @@ def tile_list_scatb_kernel(
         w_s = held("w_s", [P, 2 * N], U8)
         bias = held("bias", [P, N // P], F32)
         bias_rows = held("bias_rows", [P, P], F32)
-        win = [held(f"win{t}", [P, T], F32) for t in tiles]
+        win = [held(f"win{t}", [P, T], F32) for t in tiles[:-1]]
+        win.append(over.tile([P, T], F32, name="win3", align_bytes=64, offset=WIN3_AT))
         ones = over.tile([P, 2 * P + 2], F32, name="ones", align_bytes=64, offset=ONES_AT)
         eye = held("eye", [P, P], F32)
         sel = held("sel", [P, PACK, PACK * P], BF16)
@@ -137,7 +139,7 @@ def tile_list_scatb_kernel(
         nc.vector.memset(w_s[:].bitcast(I32), 0)
         nc.vector.memset(bias_rows[:], 0.0)
         nc.vector.memset(wgt_rows[P // 2 : P, :], 0.0)
-        for t in tiles:
+        for t in tiles[:-1]:
             nc.vector.memset(win[t][:].bitcast(I32), 0)
 
         nc.sync.dma_start(picks[:], offs)
@@ -313,6 +315,7 @@ def tile_list_scatb_kernel(
                 nc.tensor.transpose(wgt_back[h][:, u, :], wgt_wide[h][:, u].rearrange("j g r -> j (g r)"), eye[:])
         interleave_c(0)
         quantize_quarter("cq", 0)
+        nc.gpsimd.memset(win[3][:].bitcast(I32), 0)
         for h in halves:
             nc.scalar.copy(out=wgt_sb[:, h * HALF : (h + 1) * HALF], in_=wgt_back[h][:].rearrange("p u j -> p (u j)"))
 

@@ -22,6 +22,7 @@ PACK = 4
 HALF = 512
 QUARTER = 256
 STRIP = 128
+WX_ROW = 4
 GROUPS = 8
 
 QUARTER_BYTES = QUARTER * PACK * 2
@@ -86,7 +87,7 @@ def tile_list_scatb_kernel(
         wgo_sb = [held(f"wgo_sb{h}", [P, HALF], F32) for h in halves]
         wt_w = held("wt_w", [P, 2 * N], U8)
         wx_w = held("wx_w", [P, N], U32)
-        w_s = held("w_s", [P, 2 * N], U8)
+        w_s = held("w_s", [P, N], U8)
         bias = held("bias", [P, N // P], F32)
         bias_rows = held("bias_rows", [P, P], F32)
         win = [held(f"win{t}", [P, T], F32) for t in tiles[:-1]]
@@ -119,10 +120,10 @@ def tile_list_scatb_kernel(
         def load_x(i):
             nc.sync.dma_start(out=x_pl[i][:], in_=x_src[i])
 
-        def load_scales(src, column, quads):
+        def load_scales(src, row, quads):
             for quad in quads:
                 nc.sync.dma_start(
-                    out=w_s[32 * quad : 32 * quad + 4, column : column + N].bitcast(I32),
+                    out=w_s[32 * quad + row : 32 * quad + row + 4, :].bitcast(I32),
                     in_=src[0, 4 * quad : 4 * quad + 4, :].bitcast(I32),
                 )
 
@@ -149,11 +150,11 @@ def tile_list_scatb_kernel(
         load_c(0)
         load_x(0)
         nc.sync.dma_start(out=bias_rows[0 : N // P, :], in_=b.rearrange("(t p) -> t p", p=P))
-        load_scales(wx_scales, 0, (0, 1))
+        load_scales(wx_scales, WX_ROW, (0, 1))
         load_c(1)
-        load_scales(wx_scales, 0, (2, 3))
+        load_scales(wx_scales, WX_ROW, (2, 3))
         load_x(1)
-        load_scales(wt_scales, N, range(4))
+        load_scales(wt_scales, 0, range(4))
         load_x(2)
         load_x(3)
         nc.sync.dma_start(out=wt_w[:].bitcast(I32), in_=wt_words[0].bitcast(I32))
@@ -174,7 +175,8 @@ def tile_list_scatb_kernel(
                 grouped[o, lo] = xg[:, at : at + 2 * STRIP].bitcast(BF16).rearrange("p (j t) -> p j t", t=PACK)
             else:
                 grouped[o, lo] = held(f"g_{o}{lo}", [P, hi - lo, PACK], BF16, slot=slot)
-            nc.scalar.copy(
+            copy = nc.vector.tensor_copy if (o, lo) == ("cq", 0) else nc.scalar.copy
+            copy(
                 out=grouped[o, lo][:].rearrange("p (a e) t -> p a t e", e=4),
                 in_=src.rearrange("p t (a e) -> p a t e", e=4),
             )
@@ -269,9 +271,9 @@ def tile_list_scatb_kernel(
             for n, (o, at, step) in enumerate(passes):
                 h, first = divmod(at, HALF)
                 if o == "x":
-                    w, ws = wt_w[:, 2 * t * P : 2 * (t + 1) * P].bitcast(FP4X4), w_s[:, N + t * P : N + (t + 1) * P]
+                    w, ws = wt_w[:, 2 * t * P : 2 * (t + 1) * P].bitcast(FP4X4), w_s[:, ncols]
                 else:
-                    w, ws = wx_w[:, ncols].bitcast(FP8X4), w_s[:, ncols]
+                    w, ws = wx_w[:, ncols].bitcast(FP8X4), w_s[WX_ROW:P, ncols]
                 nc.tensor.matmul_mx(
                     out=acc[t, lo][:, at - lo : at - lo + step],
                     lhsT=w,
@@ -302,6 +304,7 @@ def tile_list_scatb_kernel(
         nc.scalar.copy(out=sel_words[:, 3 * plane : 4 * plane], in_=ones[:].bitcast(U32)[:, 0:plane])
         nc.scalar.copy(out=sel_words[:, plane : 2 * plane], in_=ones[:].bitcast(U32)[:, 1 : plane + 1])
         nc.scalar.copy(out=sel_words[:, 0:plane], in_=sel_words[:, 2 * plane + 1 : 3 * plane + 1])
+        interleave_c(0)
         nc.vector.quantize_mx(out=sel_w[:].bitcast(FP8X4), scales=sel_s[:], in_=sel[:].rearrange("p i m -> p (i m)"))
 
         wgt_turned = ps_dq.tile([P, P], F32, name="wgt_turned", tag=bank["wgt_turned"])
@@ -313,7 +316,6 @@ def tile_list_scatb_kernel(
             wgt_back[h] = ps_dq.tile([P, PACK, STRIP], F32, name="wgt_back", tag=bank[f"wgt_back{h}"])
             for u in range(PACK):
                 nc.tensor.transpose(wgt_back[h][:, u, :], wgt_wide[h][:, u].rearrange("j g r -> j (g r)"), eye[:])
-        interleave_c(0)
         quantize_quarter("cq", 0)
         nc.gpsimd.memset(win[3][:].bitcast(I32), 0)
         for h in halves:

@@ -31,18 +31,33 @@ WIN3_AT = 0
 CQ0_AT = WIN3_AT + 4 * T - 64
 ONES_AT = CQ0_AT + 64
 XG_AT = CQ0_AT + 832
-WIDE1_AT = XG_AT + 4 * XG_COLUMNS - 1024
 CQ3_AT = CQ0_AT + 20544
 X1_AT = CQ3_AT + QUARTER_BYTES - 64
 X_STRIP1_AT = X1_AT + QUARTER_BYTES - 512
 CQ2_AT = X1_AT + QUARTER_BYTES
 CR1_AT = CQ0_AT + 28736
+SHARED_AT = CR1_AT + QUARTER_BYTES
+SHARED = (
+    ("x_pl0", 4 * T),
+    ("x_pl1", 4 * T),
+    ("wgt_wide0", QUARTER_BYTES),
+    ("neg0", QUARTER_BYTES),
+    ("neg1", QUARTER_BYTES),
+    ("left_bf4", QUARTER_BYTES),
+    ("left_bf5", QUARTER_BYTES),
+    ("left_bf7", QUARTER_BYTES),
+)
+BANK_BYTES = 2048
 
 BANK_TENANTS = (
-    ("wgt_turned", "dq0", "left1", "dq3", "dq4", "back2"),
-    ("wgt_back0", "dq1", "back0", "left3", "left4", "dq7", "back3"),
-    ("wgt_back1", "bias_turned", "left2", "dq5", "dq6", "left7"),
-    ("left0", "dq2", "back1", "left5", "left6"),
+    ("wgt_turned", "left0", "left2", "first0", "left4", "left6"),
+    ("wgt_back0", "left1", "bias_turned", "left3", "first1", "left5", "left7"),
+    ("dq0", "dq2", "dq4", "dq6", "dq7"),
+    ("wgt_back1", "dq1", "back0", "dq3", "back1", "dq5", "back2", "back3"),
+    ("y0",),
+    ("y1",),
+    ("y2",),
+    ("y3",),
 )
 
 
@@ -50,7 +65,8 @@ def tile_list_scatb_kernel(
     tc, xT, wgt, wt_words, wt_scales, c, wx_words, wx_scales, b, wgo, offs, offs2, out
 ):
     nc = tc.nc
-    bank = {tenant: f"bank{n}" for n, tenants in enumerate(BANK_TENANTS) for tenant in tenants}
+    bank = {tenant: n * BANK_BYTES for n, tenants in enumerate(BANK_TENANTS) for tenant in tenants}
+    shared = {name: SHARED_AT + sum(size for other, size in SHARED[:n]) for n, (name, own) in enumerate(SHARED)}
     placed = {
         ("x", 0): CR1_AT,
         ("cq", 0): CQ0_AT,
@@ -65,10 +81,14 @@ def tile_list_scatb_kernel(
         keep = ctx.enter_context(tc.tile_pool(name="keep", bufs=1))
         over = ctx.enter_context(tc.tile_pool(name="over", bufs=1))
         ps_dq = ctx.enter_context(tc.psum_pool(name="ps_dq", bufs=1))
-        ps_y = ctx.enter_context(tc.psum_pool(name="ps_y", bufs=4))
 
         def held(name, shape, dtype, slot=None):
-            return keep.tile(shape, dtype, name=name, tag=slot or name, align_bytes=64)
+            if (slot or name) in shared:
+                return over.tile(shape, dtype, name=name, align_bytes=64, offset=shared[slot or name])
+            return keep.tile(shape, dtype, name=name, align_bytes=64)
+
+        def in_bank(tenant, name, shape):
+            return ps_dq.tile(shape, F32, name=name, offset=bank[tenant])
 
         picks = lists.tile([P, J // 16], U16, name="picks")
         places = lists.tile([P, J // 16], U16, name="places")
@@ -81,7 +101,7 @@ def tile_list_scatb_kernel(
         wgt_rows = held("wgt_rows", [P, STRIP], F32)
         wgt_wide = [
             held("wgt_wide0", [P, PACK, GROUPS, P // GROUPS], F32),
-            over.tile([P, PACK, GROUPS, P // GROUPS], F32, name="wgt_wide1", align_bytes=64, offset=WIDE1_AT),
+            held("wgt_wide1", [P, PACK, GROUPS, P // GROUPS], F32, slot="neg0"),
         ]
         wgt_sb = held("wgt_sb", [P, J], F32)
         wgo_sb = [held(f"wgo_sb{h}", [P, HALF], F32) for h in halves]
@@ -90,8 +110,8 @@ def tile_list_scatb_kernel(
         w_s = held("w_s", [P, N], U8)
         bias = held("bias", [P, N // P], F32)
         bias_rows = held("bias_rows", [P, P], F32)
-        win = [held(f"win{t}", [P, T], F32) for t in tiles[:-1]]
-        win.append(over.tile([P, T], F32, name="win3", align_bytes=64, offset=WIN3_AT))
+        win = {t: held(f"win{t}", [P, T], F32) for t in (0, 1)}
+        win[3] = over.tile([P, T], F32, name="win3", align_bytes=64, offset=WIN3_AT)
         ones = over.tile([P, 2 * P + 2], F32, name="ones", align_bytes=64, offset=ONES_AT)
         eye = held("eye", [P, P], F32)
         sel = held("sel", [P, PACK, PACK * P], BF16)
@@ -99,6 +119,7 @@ def tile_list_scatb_kernel(
         sel_s = held("sel_s", [P, PACK * P], U8)
         operands = ("x", "cq", "cr")
         words = {(o, h): held(f"w_{o}{h}", [P, HALF], U32) for o in operands for h in halves if (o, h) != ("cr", 0)}
+        words["cq", 0] = held("w_cq_first", [P, HALF], U32, slot="wgt_wide0")
         early_cr = {}
 
         def codes(o, lo, hi):
@@ -140,22 +161,20 @@ def tile_list_scatb_kernel(
         nc.vector.memset(w_s[:].bitcast(I32), 0)
         nc.vector.memset(bias_rows[:], 0.0)
         nc.vector.memset(wgt_rows[P // 2 : P, :], 0.0)
-        for t in tiles[:-1]:
-            nc.vector.memset(win[t][:].bitcast(I32), 0)
+        nc.vector.memset(win[0][:].bitcast(I32), 0)
 
-        nc.sync.dma_start(picks[:], offs)
         nc.sync.dma_start(
             out=wgt_rows[0 : P // 2, :], in_=wgt[0 : P : P // GROUPS, :].rearrange("g (b j) -> g b j", j=STRIP)
         )
         load_c(0)
+        nc.sync.dma_start(picks[:], offs)
         load_x(0)
-        nc.sync.dma_start(out=bias_rows[0 : N // P, :], in_=b.rearrange("(t p) -> t p", p=P))
-        load_scales(wx_scales, WX_ROW, (0, 1))
-        load_c(1)
-        load_scales(wx_scales, WX_ROW, (2, 3))
+        load_scales(wx_scales, WX_ROW, range(4))
         load_x(1)
-        load_scales(wt_scales, 0, range(4))
+        load_c(1)
+        nc.sync.dma_start(out=bias_rows[0 : N // P, :], in_=b.rearrange("(t p) -> t p", p=P))
         load_x(2)
+        load_scales(wt_scales, 0, range(4))
         load_x(3)
         nc.sync.dma_start(out=wt_w[:].bitcast(I32), in_=wt_words[0].bitcast(I32))
         nc.sync.dma_start(out=wx_w[:].bitcast(I32), in_=wx_words[0].rearrange("p n t -> p (n t)").bitcast(I32))
@@ -170,9 +189,6 @@ def tile_list_scatb_kernel(
                 grouped[o, lo] = over.tile(
                     [P, hi - lo, PACK], BF16, name=f"g_{o}{lo}", align_bytes=64, offset=placed[o, lo]
                 )
-            elif o == "cq":
-                at = xg_base[(lo - QUARTER) // STRIP] + 2 * HALF - STRIP
-                grouped[o, lo] = xg[:, at : at + 2 * STRIP].bitcast(BF16).rearrange("p (j t) -> p j t", t=PACK)
             else:
                 grouped[o, lo] = held(f"g_{o}{lo}", [P, hi - lo, PACK], BF16, slot=slot)
             copy = nc.vector.tensor_copy if (o, lo) == ("cq", 0) else nc.scalar.copy
@@ -189,15 +205,15 @@ def tile_list_scatb_kernel(
                 in_=grouped[o, lo][:].rearrange("p j t -> p (j t)"),
             )
 
-        def interleave_c(q):
-            interleave("cq", q * QUARTER, (q + 1) * QUARTER, c_raw[q][:])
+        def interleave_c(q, slot=None):
+            interleave("cq", q * QUARTER, (q + 1) * QUARTER, c_raw[q][:], slot=slot)
 
         def quantize_quarter(o, q):
             quantize(o, q * QUARTER, (q + 1) * QUARTER)
 
         def decode(s):
             h, lo = divmod(s * STRIP, HALF)
-            dq[s] = ps_dq.tile([P, PACK, STRIP], F32, name="dq", tag=bank[f"dq{s}"])
+            dq[s] = in_bank(f"dq{s}", f"dq{s}", [P, PACK, STRIP])
             for i in range(PACK):
                 nc.tensor.matmul_mx(
                     out=dq[s][:, i, :],
@@ -213,15 +229,29 @@ def tile_list_scatb_kernel(
             neg[s] = held(f"neg{s}", [P, PACK, STRIP], F32, slot=f"neg{s % 2}")
             nc.scalar.activation(out=neg[s][:], in_=dq[s][:], func=COPY, scale=-1.0)
 
-        def subtract(s):
+        def turn_c(s):
             q, lo = divmod(s * STRIP, QUARTER)
-            left[s] = ps_dq.tile([STRIP, PACK, P], F32, name="left", tag=bank[f"left{s}"])
+            left[s] = in_bank(f"left{s}", f"left{s}", [STRIP, PACK, P])
             for i in range(PACK):
-                terms = (neg[s][:, i, :], c_raw[q][:, i, lo : lo + STRIP])
-                for n, term in enumerate(terms):
-                    nc.tensor.matmul(
-                        out=left[s][:, i, :], lhsT=term, rhs=eye[:], start=(n == 0), stop=(n == 1), is_transpose=True
-                    )
+                nc.tensor.matmul(
+                    out=left[s][:, i, :],
+                    lhsT=c_raw[q][:, i, lo : lo + STRIP],
+                    rhs=eye[:],
+                    start=(i == 0),
+                    stop=False,
+                    is_transpose=True,
+                )
+
+        def subtract(s):
+            for i in range(PACK):
+                nc.tensor.matmul(
+                    out=left[s][:, i, :],
+                    lhsT=neg[s][:, i, :],
+                    rhs=eye[:],
+                    start=False,
+                    stop=(i == PACK - 1),
+                    is_transpose=True,
+                )
 
         def round_left(s):
             left_bf[s] = held(f"left_bf{s}", [STRIP, 2, P, 2], BF16)
@@ -230,7 +260,7 @@ def tile_list_scatb_kernel(
         def turn_back(s):
             q, r = divmod(s, 2)
             if r == 0:
-                back[q] = ps_dq.tile([P, 2, 2, STRIP], F32, name="back", tag=bank[f"back{q}"])
+                back[q] = in_bank(f"back{q}", f"back{q}", [P, 2, 2, STRIP])
             pairs = left_bf[s][:].rearrange("j u p e -> j (u p e)").bitcast(F32)
             for u in range(2):
                 nc.tensor.transpose(back[q][:, r, u, :], pairs[:, u * P : (u + 1) * P], eye[:])
@@ -246,9 +276,19 @@ def tile_list_scatb_kernel(
                 in_=back[q][:].rearrange("p r u j -> p r j u"),
             )
 
+        def regroup_strip(s):
+            at = xg_base[s] + 2 * HALF
+            grouped["cr", s * STRIP] = xg[:, at : at + 2 * STRIP].bitcast(BF16).rearrange("p (j t) -> p j t", t=PACK)
+            nc.scalar.copy(
+                out=xg[:, at : at + 2 * STRIP].rearrange("p (j u) -> p j u", u=2),
+                in_=back[0][:, s].rearrange("p u j -> p j u"),
+            )
+
         def decode_and_subtract(q):
             for s in (2 * q, 2 * q + 1):
                 decode(s)
+            for s in (2 * q, 2 * q + 1):
+                turn_c(s)
             for s in (2 * q, 2 * q + 1):
                 negate(s)
                 subtract(s)
@@ -259,7 +299,8 @@ def tile_list_scatb_kernel(
                 turn_back(s)
 
         def project(t, lo, hi):
-            acc[t, lo] = ps_y.tile([P, hi - lo], F32, name="acc", tag="acc")
+            tenant = f"first{t}" if lo == 0 and t < 2 else f"y{t}"
+            acc[t, lo] = in_bank(tenant, f"acc{t}_{lo}", [P, hi - lo])
             ncols = slice(t * P, (t + 1) * P)
             order = ("cr", "cq", "x") if lo == HALF else ("x", "cq", "cr") if lo < HALF else ("cq", "x", "cr")
             passes = []
@@ -297,29 +338,36 @@ def tile_list_scatb_kernel(
             if hi == J:
                 nc.sync.dma_start(out=out[t * P : (t + 1) * P, :], in_=win[t][:])
 
-        nc.scalar.copy(out=eye[:], in_=ones[:, 1 : 2 * P : 2])
-        sel_words = sel[:].rearrange("p i m -> p (i m)").bitcast(U32)
+        nc.scalar.activation(out=eye[:], in_=ones[:, 1 : 2 * P : 2], func=COPY)
+        sel_words = sel[:].rearrange("p i m -> p (i m)").bitcast(I32)
         plane = 2 * P
         nc.scalar.copy(out=sel[:, 2, :], in_=ones[:].bitcast(BF16)[:, 1 : 1 + PACK * P])
-        nc.scalar.copy(out=sel_words[:, 3 * plane : 4 * plane], in_=ones[:].bitcast(U32)[:, 0:plane])
-        nc.scalar.copy(out=sel_words[:, plane : 2 * plane], in_=ones[:].bitcast(U32)[:, 1 : plane + 1])
-        nc.scalar.copy(out=sel_words[:, 0:plane], in_=sel_words[:, 2 * plane + 1 : 3 * plane + 1])
+        nc.vector.tensor_copy(out=sel_words[:, 3 * plane : 4 * plane], in_=ones[:].bitcast(I32)[:, 0:plane])
+        nc.vector.tensor_copy(out=sel_words[:, plane : 2 * plane], in_=ones[:].bitcast(I32)[:, 1 : plane + 1])
+        nc.vector.memset(win[1][:].bitcast(I32), 0)
+        nc.vector.tensor_copy(out=sel_words[:, 0:plane], in_=sel_words[:, 2 * plane + 1 : 3 * plane + 1])
         interleave_c(0)
         nc.vector.quantize_mx(out=sel_w[:].bitcast(FP8X4), scales=sel_s[:], in_=sel[:].rearrange("p i m -> p (i m)"))
 
-        wgt_turned = ps_dq.tile([P, P], F32, name="wgt_turned", tag=bank["wgt_turned"])
+        wgt_turned = in_bank("wgt_turned", "wgt_turned", [P, P])
         nc.tensor.transpose(wgt_turned[:], wgt_rows[:], eye[:])
         wgt_back = {}
         for h in halves:
-            strips = wgt_turned[:, 0 : P // 2].rearrange("j (g b) -> j b g", g=GROUPS)[:, h * PACK : (h + 1) * PACK, :]
-            nc.scalar.copy(out=wgt_wide[h][:], in_=strips.unsqueeze(3).to_broadcast([P, PACK, GROUPS, P // GROUPS]))
-            wgt_back[h] = ps_dq.tile([P, PACK, STRIP], F32, name="wgt_back", tag=bank[f"wgt_back{h}"])
+            strips = wgt_turned[:, 0 : P // 2].rearrange("j (g a h e) -> j h a e g", g=GROUPS, a=2, h=2)[:, h]
+            nc.scalar.copy(
+                out=wgt_wide[h][:].rearrange("j (a e) g r -> j a e g r", a=2),
+                in_=strips.unsqueeze(4).to_broadcast([P, 2, 2, GROUPS, P // GROUPS]),
+            )
+            wgt_back[h] = in_bank(f"wgt_back{h}", f"wgt_back{h}", [P, PACK, STRIP])
             for u in range(PACK):
                 nc.tensor.transpose(wgt_back[h][:, u, :], wgt_wide[h][:, u].rearrange("j g r -> j (g r)"), eye[:])
         quantize_quarter("cq", 0)
         nc.gpsimd.memset(win[3][:].bitcast(I32), 0)
         for h in halves:
-            nc.scalar.copy(out=wgt_sb[:, h * HALF : (h + 1) * HALF], in_=wgt_back[h][:].rearrange("p u j -> p (u j)"))
+            nc.scalar.copy(
+                out=wgt_sb[:].rearrange("p (a h j) -> p h a j", a=2, h=2)[:, h],
+                in_=wgt_back[h][:].rearrange("p (a e) j -> p a (e j)", a=2),
+            )
 
         xg = over.tile([P, XG_COLUMNS], F32, name="xg", align_bytes=64, offset=XG_AT)
         xg_base = (PACK * HALF - STRIP, 0)
@@ -338,31 +386,26 @@ def tile_list_scatb_kernel(
             h, at = divmod(lo, HALF)
             interleave("x", lo, hi, xg_half[h][:, :, at : at + hi - lo], slot=slot)
 
-        gather(0, 0, HALF)
+        gather(0, 0, QUARTER)
+        gather(0, QUARTER, HALF)
         gather(0, HALF, J)
+        win[2] = held("win2", [P, T], F32, slot="x_pl0")
+        nc.gpsimd.memset(win[2][:].bitcast(I32), 0)
         decode_and_subtract(0)
-        bias_turned = ps_dq.tile([P, P], F32, name="bias_turned", tag=bank["bias_turned"])
-        nc.tensor.transpose(bias_turned[:], bias_rows[:], eye[:])
-        nc.scalar.copy(out=bias[:], in_=bias_turned[:, 0 : N // P])
-        for lo in (QUARTER, QUARTER + STRIP):
-            interleave("cq", lo, lo + STRIP, c_raw[1][:, :, lo - QUARTER : lo - QUARTER + STRIP])
-            quantize("cq", lo, lo + STRIP)
-        round_left(0)
-        decode(2)
-        decode(3)
-        round_left(1)
-        turn_back(0)
-        turn_back(1)
-        negate(2)
-        negate(3)
-        regroup(0)
-        subtract(2)
-        subtract(3)
         gather(1, 0, HALF)
         gather(1, HALF, J)
-        gather(2, 0, HALF)
+        round_and_turn(0)
+        bias_turned = in_bank("bias_turned", "bias_turned", [P, P])
+        nc.tensor.transpose(bias_turned[:], bias_rows[:], eye[:])
+        nc.scalar.copy(out=bias[:], in_=bias_turned[:, 0 : N // P])
+        interleave_c(1, slot="neg1")
+        quantize_quarter("cq", 1)
         early_cr[0] = held("w_cr_early0", [P, QUARTER], U32, slot="x_pl1")
-        quantize_quarter("cr", 0)
+        for s in (0, 1):
+            regroup_strip(s)
+            quantize("cr", s * STRIP, (s + 1) * STRIP)
+        decode_and_subtract(1)
+        gather(2, 0, HALF)
         gather(2, HALF, J)
 
         last = PACK - 1

from contextlib import ExitStack

import concourse.mybir as mybir

K, L, N, T, J = 512, 512, 512, 2048, 1024
FLOPS = 2 * J * (K * N + 2 * L * N + L * L)

F32 = mybir.dt.float32
BF16 = mybir.dt.bfloat16
I32 = mybir.dt.int32
U32 = mybir.dt.uint32
U16 = mybir.dt.uint16
U8 = mybir.dt.uint8
FP8X4 = mybir.dt.float8_e4m3fn_x4
FP4X4 = mybir.dt.float4_e2m1fn_x4
MULT = mybir.AluOpType.mult
COPY = mybir.ActivationFunctionType.Copy
IDENT = mybir.ActivationFunctionType.Identity

P = 128
PACK = 4
HALF = 512
QUARTER = 256
STRIP = 128
WX_ROW = 4
GROUPS = 8

QUARTER_BYTES = QUARTER * PACK * 2
XG_COLUMNS = PACK * J - STRIP
WIN3_AT = 0
CQ0_AT = WIN3_AT + 4 * T - 64
ONES_AT = CQ0_AT + 64
XG_AT = CQ0_AT + 832
CQ3_AT = CQ0_AT + 20544
X1_AT = CQ3_AT + QUARTER_BYTES - 64
X_STRIP1_AT = X1_AT + QUARTER_BYTES - 512
CQ2_AT = X1_AT + QUARTER_BYTES
CR1_AT = CQ0_AT + 28736
SHARED_AT = CR1_AT + QUARTER_BYTES
SHARED = (
    ("x_pl0", 4 * T),
    ("x_pl1", 4 * T),
    ("wgt_wide0", QUARTER_BYTES),
    ("neg0", QUARTER_BYTES),
    ("neg1", QUARTER_BYTES),
    ("left_bf4", QUARTER_BYTES),
    ("left_bf5", QUARTER_BYTES),
    ("left_bf7", QUARTER_BYTES),
)
BANK_BYTES = 2048

BANK_TENANTS = (
    ("wgt_turned", "left0", "left2", "first0", "left4", "left6"),
    ("wgt_back0", "left1", "bias_turned", "left3", "first1", "left5", "left7"),
    ("dq0", "dq2", "dq4", "dq6", "dq7"),
    ("wgt_back1", "dq1", "back0", "dq3", "back1", "dq5", "back2", "back3"),
    ("y0",),
    ("y1",),
    ("y2",),
    ("y3",),
)


def tile_list_scatb_kernel(
    tc, xT, wgt, wt_words, wt_scales, c, wx_words, wx_scales, b, wgo, offs, offs2, out
):
    nc = tc.nc
    bank = {tenant: n * BANK_BYTES for n, tenants in enumerate(BANK_TENANTS) for tenant in tenants}
    shared = {name: SHARED_AT + sum(size for other, size in SHARED[:n]) for n, (name, own) in enumerate(SHARED)}
    placed = {
        ("x", 0): CR1_AT,
        ("cq", 0): CQ0_AT,
        ("cq", 3 * QUARTER): CQ3_AT,
        ("x", QUARTER): X1_AT,
        ("x", STRIP): X_STRIP1_AT,
        ("cq", 2 * QUARTER): CQ2_AT,
        ("x", 2 * QUARTER): CQ2_AT,
    }
    with ExitStack() as ctx:
        lists = ctx.enter_context(tc.tile_pool(name="lists", bufs=1))
        keep = ctx.enter_context(tc.tile_pool(name="keep", bufs=1))
        over = ctx.enter_context(tc.tile_pool(name="over", bufs=1))
        ps_dq = ctx.enter_context(tc.psum_pool(name="ps_dq", bufs=1))

        def held(name, shape, dtype, slot=None):
            if (slot or name) in shared:
                return over.tile(shape, dtype, name=name, align_bytes=64, offset=shared[slot or name])
            return keep.tile(shape, dtype, name=name, align_bytes=64)

        def in_bank(tenant, name, shape):
            return ps_dq.tile(shape, F32, name=name, offset=bank[tenant])

        picks = lists.tile([P, J // 16], U16, name="picks")
        places = lists.tile([P, J // 16], U16, name="places")
        halves = range(J // HALF)
        quarters = range(J // QUARTER)
        tiles = range(N // P)

        x_pl = [held(f"x_pl{i}", [P, T], F32) for i in range(PACK)]
        c_raw = [held(f"c_raw{q}", [P, PACK, QUARTER], F32) for q in quarters]
        wgt_rows = held("wgt_rows", [P, STRIP], F32)
        wgt_wide = [
            held("wgt_wide0", [P, PACK, GROUPS, P // GROUPS], F32),
            held("wgt_wide1", [P, PACK, GROUPS, P // GROUPS], F32, slot="neg0"),
        ]
        wgt_sb = held("wgt_sb", [P, J], F32)
        wgo_sb = [held(f"wgo_sb{h}", [P, HALF], F32) for h in halves]
        wt_w = held("wt_w", [P, 2 * N], U8)
        wx_w = held("wx_w", [P, N], U32)
        w_s = held("w_s", [P, N], U8)
        bias = held("bias", [P, N // P], F32)
        bias_rows = held("bias_rows", [P, P], F32)
        win = {t: held(f"win{t}", [P, T], F32) for t in (0, 1)}
        win[3] = over.tile([P, T], F32, name="win3", align_bytes=64, offset=WIN3_AT)
        ones = over.tile([P, 2 * P + 2], F32, name="ones", align_bytes=64, offset=ONES_AT)
        eye = held("eye", [P, P], F32)
        sel = held("sel", [P, PACK, PACK * P], BF16)
        sel_w = held("sel_w", [P, PACK * P], U32)
        sel_s = held("sel_s", [P, PACK * P], U8)
        operands = ("x", "cq", "cr")
        words = {(o, h): held(f"w_{o}{h}", [P, HALF], U32) for o in operands for h in halves if (o, h) != ("cr", 0)}
        words["cq", 0] = held("w_cq_first", [P, HALF], U32, slot="wgt_wide0")
        early_cr = {}

        def codes(o, lo, hi):
            if o == "cr" and lo < HALF:
                q, at = divmod(lo, QUARTER)
                return early_cr[q][:, at : at + hi - lo].bitcast(FP8X4)
            h, at = divmod(lo, HALF)
            return words[o, h][:, at : at + hi - lo].bitcast(FP8X4)

        scales = {(o, h): held(f"s_{o}{h}", [P, HALF], U8) for o in operands for h in halves}
        grouped, ys, acc, dq, neg, left, left_bf, back = {}, {}, {}, {}, {}, {}, {}, {}

        x_src = xT.rearrange("(p i) t -> i p t", i=PACK)
        c_src = c.rearrange("(p i) j -> p i j", i=PACK)

        def load_c(q):
            nc.sync.dma_start(out=c_raw[q][:], in_=c_src[:, :, q * QUARTER : (q + 1) * QUARTER])

        def load_x(i):
            nc.sync.dma_start(out=x_pl[i][:], in_=x_src[i])

        def load_scales(src, row, quads):
            for quad in quads:
                nc.sync.dma_start(
                    out=w_s[32 * quad + row : 32 * quad + row + 4, :].bitcast(I32),
                    in_=src[0, 4 * quad : 4 * quad + 4, :].bitcast(I32),
                )

        nc.gpsimd.memset(ones[:], 0.0)
        nc.gpsimd.affine_select(
            out=ones[:],
            in_=ones[:],
            pattern=[[1, 2 * P + 2]],
            compare_op=mybir.AluOpType.not_equal,
            fill=1.0,
            base=-1,
            channel_multiplier=-2,
        )
        nc.vector.memset(w_s[:].bitcast(I32), 0)
        nc.vector.memset(bias_rows[:], 0.0)
        nc.vector.memset(wgt_rows[P // 2 : P, :], 0.0)
        nc.vector.memset(win[0][:].bitcast(I32), 0)

        nc.sync.dma_start(
            out=wgt_rows[0 : P // 2, :], in_=wgt[0 : P : P // GROUPS, :].rearrange("g (b j) -> g b j", j=STRIP)
        )
        load_c(0)
        nc.sync.dma_start(picks[:], offs)
        load_x(0)
        load_scales(wx_scales, WX_ROW, range(4))
        load_x(1)
        load_c(1)
        nc.sync.dma_start(out=bias_rows[0 : N // P, :], in_=b.rearrange("(t p) -> t p", p=P))
        load_x(2)
        load_scales(wt_scales, 0, range(4))
        load_x(3)
        nc.sync.dma_start(out=wt_w[:].bitcast(I32), in_=wt_words[0].bitcast(I32))
        nc.sync.dma_start(out=wx_w[:].bitcast(I32), in_=wx_words[0].rearrange("p n t -> p (n t)").bitcast(I32))
        nc.sync.dma_start(places[:], offs2)
        nc.sync.dma_start(out=wgo_sb[0][:], in_=wgo[:, 0:HALF])
        load_c(2)
        load_c(3)
        nc.sync.dma_start(out=wgo_sb[1][:], in_=wgo[:, HALF:J])

        def interleave(o, lo, hi, src, slot=None):
            if (o, lo) in placed:
                grouped[o, lo] = over.tile(
                    [P, hi - lo, PACK], BF16, name=f"g_{o}{lo}", align_bytes=64, offset=placed[o, lo]
                )
            else:
                grouped[o, lo] = held(f"g_{o}{lo}", [P, hi - lo, PACK], BF16, slot=slot)
            copy = nc.vector.tensor_copy if (o, lo) == ("cq", 0) else nc.scalar.copy
            copy(
                out=grouped[o, lo][:].rearrange("p (a e) t -> p a t e", e=4),
                in_=src.rearrange("p t (a e) -> p a t e", e=4),
            )

        def quantize(o, lo, hi):
            h, at = divmod(lo, HALF)
            nc.vector.quantize_mx(
                out=codes(o, lo, hi),
                scales=scales[o, h][:, at : at + hi - lo],
                in_=grouped[o, lo][:].rearrange("p j t -> p (j t)"),
            )

        def interleave_c(q, slot=None):
            interleave("cq", q * QUARTER, (q + 1) * QUARTER, c_raw[q][:], slot=slot)

        def quantize_quarter(o, q):
            quantize(o, q * QUARTER, (q + 1) * QUARTER)

        def decode(s):
            h, lo = divmod(s * STRIP, HALF)
            dq[s] = in_bank(f"dq{s}", f"dq{s}", [P, PACK, STRIP])
            for i in range(PACK):
                nc.tensor.matmul_mx(
                    out=dq[s][:, i, :],
                    lhsT=sel_w[:, i * P : (i + 1) * P].bitcast(FP8X4),
                    lhsT_scale=sel_s[:, i * P : (i + 1) * P],
                    rhs=words["cq", h][:, lo : lo + STRIP].bitcast(FP8X4),
                    rhs_scale=scales["cq", h][:, lo : lo + STRIP],
                    start=True,
                    stop=True,
                )

        def negate(s):
            neg[s] = held(f"neg{s}", [P, PACK, STRIP], F32, slot=f"neg{s % 2}")
            nc.scalar.activation(out=neg[s][:], in_=dq[s][:], func=COPY, scale=-1.0)

        def turn_c(s):
            q, lo = divmod(s * STRIP, QUARTER)
            left[s] = in_bank(f"left{s}", f"left{s}", [STRIP, PACK, P])
            for i in range(PACK):
                nc.tensor.matmul(
                    out=left[s][:, i, :],
                    lhsT=c_raw[q][:, i, lo : lo + STRIP],
                    rhs=eye[:],
                    start=(i == 0),
                    stop=False,
                    is_transpose=True,
                )

        def subtract(s):
            for i in range(PACK):
                nc.tensor.matmul(
                    out=left[s][:, i, :],
                    lhsT=neg[s][:, i, :],
                    rhs=eye[:],
                    start=False,
                    stop=(i == PACK - 1),
                    is_transpose=True,
                )

        def round_left(s):
            left_bf[s] = held(f"left_bf{s}", [STRIP, 2, P, 2], BF16)
            nc.scalar.copy(out=left_bf[s][:], in_=left[s][:].rearrange("j (u e) p -> j u p e", u=2))

        def turn_back(s):
            q, r = divmod(s, 2)
            if r == 0:
                back[q] = in_bank(f"back{q}", f"back{q}", [P, 2, 2, STRIP])
            pairs = left_bf[s][:].rearrange("j u p e -> j (u p e)").bitcast(F32)
            for u in range(2):
                nc.tensor.transpose(back[q][:, r, u, :], pairs[:, u * P : (u + 1) * P], eye[:])

        def regroup(q):
            if q == 1:
                dst = over.tile([P, QUARTER, PACK], BF16, name="g_cr1", align_bytes=64, offset=CR1_AT)
            else:
                dst = held(f"g_cr{q}", [P, QUARTER, PACK], BF16)
            grouped["cr", q * QUARTER] = dst
            nc.scalar.copy(
                out=dst[:].bitcast(F32).rearrange("p (r j) u -> p r j u", r=2),
                in_=back[q][:].rearrange("p r u j -> p r j u"),
            )

        def regroup_strip(s):
            at = xg_base[s] + 2 * HALF
            grouped["cr", s * STRIP] = xg[:, at : at + 2 * STRIP].bitcast(BF16).rearrange("p (j t) -> p j t", t=PACK)
            nc.scalar.copy(
                out=xg[:, at : at + 2 * STRIP].rearrange("p (j u) -> p j u", u=2),
                in_=back[0][:, s].rearrange("p u j -> p j u"),
            )

        def decode_and_subtract(q):
            for s in (2 * q, 2 * q + 1):
                decode(s)
            for s in (2 * q, 2 * q + 1):
                turn_c(s)
            for s in (2 * q, 2 * q + 1):
                negate(s)
                subtract(s)

        def round_and_turn(q):
            for s in (2 * q, 2 * q + 1):
                round_left(s)
                turn_back(s)

        def project(t, lo, hi):
            tenant = f"first{t}" if lo == 0 and t < 2 else f"y{t}"
            acc[t, lo] = in_bank(tenant, f"acc{t}_{lo}", [P, hi - lo])
            ncols = slice(t * P, (t + 1) * P)
            order = ("cr", "cq", "x") if lo == HALF else ("x", "cq", "cr") if lo < HALF else ("cq", "x", "cr")
            passes = []
            for o in order:
                if lo % QUARTER and hi - lo > STRIP:
                    passes.extend([(o, lo, STRIP), (o, lo + STRIP, QUARTER)])
                else:
                    passes.append((o, lo, hi - lo))
            for n, (o, at, step) in enumerate(passes):
                h, first = divmod(at, HALF)
                if o == "x":
                    w, ws = wt_w[:, 2 * t * P : 2 * (t + 1) * P].bitcast(FP4X4), w_s[:, ncols]
                else:
                    w, ws = wx_w[:, ncols].bitcast(FP8X4), w_s[WX_ROW:P, ncols]
                nc.tensor.matmul_mx(
                    out=acc[t, lo][:, at - lo : at - lo + step],
                    lhsT=w,
                    lhsT_scale=ws,
                    rhs=codes(o, at, at + step),
                    rhs_scale=scales[o, h][:, first : first + step],
                    start=(n == 0),
                    stop=(n == len(passes) - 1),
                )

        def finish(t, lo, hi, slot=None):
            ys[t, lo] = held(f"ys{t}_{lo}", [P, hi - lo], F32, slot=slot)
            nc.scalar.activation(out=ys[t, lo][:], in_=acc[t, lo][:], func=IDENT, bias=bias[:, t : t + 1], scale=1.0)
            h, at = divmod(lo, HALF)
            nc.vector.tensor_tensor(
                win[t][:].indirect(places[:, lo // 16 : hi // 16]),
                ys[t, lo][:],
                wgo_sb[h][:, at : at + hi - lo],
                MULT,
            )
            if hi == J:
                nc.sync.dma_start(out=out[t * P : (t + 1) * P, :], in_=win[t][:])

        nc.scalar.activation(out=eye[:], in_=ones[:, 1 : 2 * P : 2], func=COPY)
        sel_words = sel[:].rearrange("p i m -> p (i m)").bitcast(I32)
        plane = 2 * P
        nc.scalar.copy(out=sel[:, 2, :], in_=ones[:].bitcast(BF16)[:, 1 : 1 + PACK * P])
        nc.vector.tensor_copy(out=sel_words[:, 3 * plane : 4 * plane], in_=ones[:].bitcast(I32)[:, 0:plane])
        nc.vector.tensor_copy(out=sel_words[:, plane : 2 * plane], in_=ones[:].bitcast(I32)[:, 1 : plane + 1])
        nc.vector.memset(win[1][:].bitcast(I32), 0)
        nc.vector.tensor_copy(out=sel_words[:, 0:plane], in_=sel_words[:, 2 * plane + 1 : 3 * plane + 1])
        interleave_c(0)
        nc.vector.quantize_mx(out=sel_w[:].bitcast(FP8X4), scales=sel_s[:], in_=sel[:].rearrange("p i m -> p (i m)"))

        wgt_turned = in_bank("wgt_turned", "wgt_turned", [P, P])
        nc.tensor.transpose(wgt_turned[:], wgt_rows[:], eye[:])
        wgt_back = {}
        for h in halves:
            strips = wgt_turned[:, 0 : P // 2].rearrange("j (g a h e) -> j h a e g", g=GROUPS, a=2, h=2)[:, h]
            nc.scalar.copy(
                out=wgt_wide[h][:].rearrange("j (a e) g r -> j a e g r", a=2),
                in_=strips.unsqueeze(4).to_broadcast([P, 2, 2, GROUPS, P // GROUPS]),
            )
            wgt_back[h] = in_bank(f"wgt_back{h}", f"wgt_back{h}", [P, PACK, STRIP])
            for u in range(PACK):
                nc.tensor.transpose(wgt_back[h][:, u, :], wgt_wide[h][:, u].rearrange("j g r -> j (g r)"), eye[:])
        quantize_quarter("cq", 0)
        nc.gpsimd.memset(win[3][:].bitcast(I32), 0)
        for h in halves:
            nc.scalar.copy(
                out=wgt_sb[:].rearrange("p (a h j) -> p h a j", a=2, h=2)[:, h],
                in_=wgt_back[h][:].rearrange("p (a e) j -> p a (e j)", a=2),
            )

        xg = over.tile([P, XG_COLUMNS], F32, name="xg", align_bytes=64, offset=XG_AT)
        xg_base = (PACK * HALF - STRIP, 0)
        xg_half = [xg[:, at : at + PACK * HALF].rearrange("p (i j) -> p i j", i=PACK) for at in xg_base]

        def gather(i, lo, hi):
            h, at = divmod(lo, HALF)
            nc.vector.tensor_tensor(
                xg_half[h][:, i, at : at + hi - lo],
                x_pl[i][:].indirect(picks[:, lo // 16 : hi // 16]),
                wgt_sb[:, lo:hi],
                MULT,
            )

        def interleave_x(lo, hi, slot=None):
            h, at = divmod(lo, HALF)
            interleave("x", lo, hi, xg_half[h][:, :, at : at + hi - lo], slot=slot)

        gather(0, 0, QUARTER)
        gather(0, QUARTER, HALF)
        gather(0, HALF, J)
        win[2] = held("win2", [P, T], F32, slot="x_pl0")
        nc.gpsimd.memset(win[2][:].bitcast(I32), 0)
        decode_and_subtract(0)
        gather(1, 0, HALF)
        gather(1, HALF, J)
        round_and_turn(0)
        bias_turned = in_bank("bias_turned", "bias_turned", [P, P])
        nc.tensor.transpose(bias_turned[:], bias_rows[:], eye[:])
        nc.scalar.copy(out=bias[:], in_=bias_turned[:, 0 : N // P])
        interleave_c(1, slot="neg1")
        quantize_quarter("cq", 1)
        early_cr[0] = held("w_cr_early0", [P, QUARTER], U32, slot="x_pl1")
        for s in (0, 1):
            regroup_strip(s)
            quantize("cr", s * STRIP, (s + 1) * STRIP)
        decode_and_subtract(1)
        gather(2, 0, HALF)
        gather(2, HALF, J)

        last = PACK - 1
        gather(last, 0, STRIP)
        gather(last, STRIP, HALF)
        round_and_turn(1)
        interleave_x(0, STRIP)
        quantize("x", 0, STRIP)
        gather(last, HALF, J)
        interleave_x(STRIP, QUARTER)
        quantize("x", STRIP, QUARTER)
        for t in tiles:
            project(t, 0, STRIP)
        regroup(1)
        early_cr[1] = held("w_cr_early1", [P, QUARTER], U32)
        quantize_quarter("cr", 1)
        finish(0, 0, STRIP)
        finish(1, 0, STRIP)
        interleave_x(QUARTER, HALF)
        quantize_quarter("x", 1)
        finish(2, 0, STRIP)
        finish(3, 0, STRIP)

        for t in tiles:
            project(t, STRIP, HALF)
        interleave_c(2)
        quantize_quarter("cq", 2)
        finish(0, STRIP, HALF)
        interleave_c(3)
        quantize_quarter("cq", 3)
        finish(1, STRIP, HALF)
        decode_and_subtract(2)
        interleave_x(2 * QUARTER, 3 * QUARTER)
        quantize_quarter("x", 2)
        round_and_turn(2)
        finish(2, STRIP, HALF)
        decode_and_subtract(3)
        regroup(2)
        quantize_quarter("cr", 2)
        finish(3, STRIP, HALF, slot="left_bf5")

        for t in (0, 1):
            project(t, HALF, 3 * QUARTER)
        interleave_x(3 * QUARTER, J, slot="left_bf4")
        quantize_quarter("x", 3)
        finish(0, HALF, 3 * QUARTER)
        round_and_turn(3)
        regroup(3)
        quantize_quarter("cr", 3)
        finish(1, HALF, 3 * QUARTER, slot="left_bf7")
        for t in (0, 1):
            project(t, 3 * QUARTER, J)
            finish(t, 3 * QUARTER, J)
        for t in (2, 3):
            project(t, HALF, J)
            finish(t, HALF, J)
